import numpy as np
import ml_dtypes


def mxq(x, axis, fmt="e4m3"):
    dtype, down = {"e4m3": (ml_dtypes.float8_e4m3fn, 7), "e5m2": (ml_dtypes.float8_e5m2, 14)}[fmt]
    v = np.moveaxis(np.asarray(x, np.float32).astype(ml_dtypes.bfloat16).astype(np.float64), axis, -1)
    blocks = v.reshape(v.shape[:-1] + (-1, 32))
    amax = np.abs(blocks).max(-1, keepdims=True)
    byte = np.maximum(np.where(amax > 0, np.frexp(amax)[1] - 1 + 127, 0) - down, 1)
    scale = np.exp2(byte - 127.0)
    codes = (blocks / scale).astype(np.float32).astype(dtype).astype(np.float64)
    return np.moveaxis((codes * scale).reshape(v.shape), -1, axis)


WIDE = False


def mx_kscale(k):
    if not WIDE:
        return np.ones(k)
    levels = np.array([10, -10, 5, -5, 0])
    if k % 512:
        return np.exp2(np.random.permutation(np.resize(levels, k // 32))).repeat(32)
    a = np.empty((k // 512, 16))
    for p in range(k // 512):
        a[p, :8] = np.random.permutation(np.resize(levels, 8))
        for g in range(8):
            far = levels[np.abs(levels - a[p, g]) >= 10]
            a[p, g + 8] = far[np.random.randint(len(far))]
    return np.exp2(a.ravel()).repeat(32)


def f64(x):
    return np.asarray(x).astype(np.float64)


def striped(idx):
    return np.tile(idx.reshape(-1, 16).T, (8, 1)).astype(np.uint16)


def unstriped(offs):
    return offs[:16].T.reshape(-1).astype(np.int64)


E2M1 = np.array([0.0, 0.5, 1.0, 1.5, 2.0, 3.0, 4.0, 6.0, -0.0, -0.5, -1.0, -1.5, -2.0, -3.0, -4.0, -6.0])


def pack_weight(w, fmt):
    k, n = w.shape
    w = f64(np.asarray(w, np.float32).astype(ml_dtypes.bfloat16)).reshape(k // 32, 32, n)
    amax = np.abs(w).max(1)
    if fmt == "e4m3":
        byte = np.frexp(amax)[1] - 1 + 127 - 7
    else:
        mant, ex = np.frexp(amax / 6.0)
        byte = np.where(mant > 0.5, ex, ex - 1) + 127
    byte = np.clip(np.where(amax > 0, byte, 1), 1, 254)
    scaled = (w * np.exp2(127.0 - byte)[:, None, :]).reshape(k, n).astype(np.float32)
    by_word = np.ascontiguousarray(scaled.reshape(k // 512, 128, 4, n).transpose(0, 1, 3, 2))
    if fmt == "e4m3":
        words = by_word.astype(ml_dtypes.float8_e4m3fn).view(np.uint8)
    else:
        c = by_word.astype(ml_dtypes.float4_e2m1fn).view(np.uint8) & 0xF
        words = (c[..., 0::2] | (c[..., 1::2] << 4)).reshape(k // 512, 128, 2 * n)
    return np.ascontiguousarray(words), np.ascontiguousarray(byte.astype(np.uint8).reshape(k // 512, 16, n))


def unpack_weight(words, scales, fmt):
    g, _, n = scales.shape
    words = np.ascontiguousarray(words).reshape(g, 128, n, -1)
    if fmt == "e4m3":
        vals = words.view(ml_dtypes.float8_e4m3fn).astype(np.float64)
    else:
        nib = np.empty((g, 128, n, 4), np.uint8)
        nib[..., 0::2] = words & 0xF
        nib[..., 1::2] = words >> 4
        vals = E2M1[nib]
    vals = vals * np.repeat(np.exp2(scales.astype(np.float64) - 127.0), 8, axis=1)[..., None]
    return vals.transpose(0, 1, 3, 2).reshape(g * 512, n)


def gelu(v):
    return 0.5 * v * (1.0 + np.tanh(np.sqrt(2.0 / np.pi) * (v + 0.044715 * v**3)))


K, T, S, P, H, N = 1024, 4096, 1024, 512, 1024, 512

def setup_inputs():
    n = np.random.standard_normal
    s = mx_kscale(K)[:, None]
    u = mx_kscale(H)[:, None]
    tab_words, tab_scales = pack_weight(n((K, T)) * s, "e4m3")
    phase = 3.0 * n((K, H))
    we = np.sqrt(2.0 / K) * np.cos(phase) / s * u.T
    wo = np.sqrt(2.0 / K) * np.sin(phase) / s * u.T
    w2_words, w2_scales = pack_weight(n((H, N)) / np.sqrt(H) / u, "e2m1")
    return {
        "tab_words": tab_words, "tab_scales": tab_scales,
        "offs": striped(np.random.permutation(T)[:S]),
        "we": we.astype(np.float32),
        "wo": wo.astype(np.float32),
        "pos1": striped(np.random.permutation(S)[:P]),
        "pos2": striped(np.random.permutation(S)[:P]),
        "w2_words": w2_words, "w2_scales": w2_scales,
    }

def reference(tab_words, tab_scales, offs, we, wo, pos1, pos2, w2_words, w2_scales):
    v = unpack_weight(tab_words, tab_scales, "e4m3")[:, unstriped(offs)]
    e = mxq(f64(we), 0, "e4m3").T @ v
    o = mxq(f64(wo), 0, "e4m3").T @ v
    h = np.sqrt(e * e + o * o)
    a = h[:, unstriped(pos1)]
    b = h[:, unstriped(pos2)]
    z = a - b
    w2 = unpack_weight(w2_words, w2_scales, "e2m1")
    return w2.T @ mxq(z, 0, "e4m3")

@@ -1,0 +1,240 @@
+from contextlib import ExitStack
+
+import concourse.mybir as mybir
+
+K, T, S, NPAIR, H, N = 1024, 4096, 1024, 512, 1024, 512
+FLOPS = 2 * 2 * K * H * S + 2 * H * N * NPAIR
+
+F32 = mybir.dt.float32
+BF16 = mybir.dt.bfloat16
+I32 = mybir.dt.int32
+U32 = mybir.dt.uint32
+U16 = mybir.dt.uint16
+U8 = mybir.dt.uint8
+FP8X4 = mybir.dt.float8_e4m3fn_x4
+FP4X4 = mybir.dt.float4_e2m1fn_x4
+ACT = mybir.ActivationFunctionType
+ALU = mybir.AluOpType
+
+P = 128
+PACK = 4
+KP = P * PACK
+BANK = 512
+CAST_ON = {"e00": "s", "e10": "s", "o00": "v", "o10": "vv", "e01": "s", "e11": "s", "o01": "s", "o11": "s"}
+ADD_ON = ["v"] * 8
+SUB_ON = "vv"
+TAIL = 4
+SPLIT_LAST = 2
+
+
+def tile_list_quadrature_motion_readout_kernel(
+    tc, tab_words, tab_scales, offs, we, wo, pos1, pos2, w2_words, w2_scales, out
+):
+    nc = tc.nc
+    with ExitStack() as ctx:
+        keep = ctx.enter_context(tc.tile_pool(name="keep", bufs=1))
+        ring = ctx.enter_context(tc.tile_pool(name="ring", bufs=2))
+        psum = ctx.enter_context(tc.psum_pool(name="psum", bufs=8))
+
+        offs_t = keep.tile([P, S // 16], U16, name="offs_t")
+        pos1_t = keep.tile([P, NPAIR // 16], U16, name="pos1_t")
+        pos2_t = keep.tile([P, NPAIR // 16], U16, name="pos2_t")
+        tab_t = [keep.tile([P, T], I32, name="tab%d" % a, align_bytes=64) for a in range(2)]
+        tabs_t = keep.tile([P, T // 4], I32, name="tabs", align_bytes=64)
+        w2_t = keep.tile([P, 2, 2 * N], U8, name="w2w", align_bytes=64)
+        w2s_t = keep.tile([P, 2, N], U8, name="w2s", align_bytes=64)
+        v_t = [keep.tile([P, S], U32, name="v%d" % a, align_bytes=64) for a in range(2)]
+        vs_t = keep.tile([P, S], U8, name="vs", align_bytes=64)
+        zero = keep.tile([P, 1], F32, name="zero")
+        bias0 = keep.tile([P, 1], F32, name="bias0")
+        w_in = {"e": we, "o": wo}
+        raw, codes, scales = {}, {}, {}
+        for m in "eo":
+            for a in range(2):
+                for b in range(2):
+                    key = (m, a, b)
+                    codes[key] = keep.tile([P, KP], U32, name="wc%s%d%d" % key, align_bytes=64)
+                    scales[key] = keep.tile([P, KP], U8, name="ws%s%d%d" % key, align_bytes=64)
+        z_codes = [keep.tile([P, NPAIR], U32, name="zc%d" % b, align_bytes=64) for b in range(2)]
+        z_scales = [keep.tile([P, NPAIR], U8, name="zs%d" % b, align_bytes=64) for b in range(2)]
+
+        nc.vector.memset(tabs_t[:], 0)
+        nc.vector.memset(zero[:], 0.0)
+        nc.vector.memset(w2s_t[:].rearrange("p a n -> p (a n)").bitcast(I32), 0)
+        nc.scalar.activation(out=bias0[:], in_=zero[:], func=ACT.Sqrt)
+
+        def load_w(key, parts=1):
+            m, a, b = key
+            width = KP // parts
+            raw[key] = ring.tile([P, PACK, KP], F32, name="raw", tag="raw", bufs=6, align_bytes=64)
+            for h in range(parts):
+                src = w_in[m][a * KP : (a + 1) * KP, b * KP + h * width : b * KP + (h + 1) * width]
+                nc.sync.dma_start(
+                    out=raw[key][:, :, h * width : (h + 1) * width],
+                    in_=src.rearrange("(p j) r -> p j r", j=PACK),
+                )
+
+        def load_tab(a):
+            nc.sync.dma_start(out=tab_t[a][:], in_=tab_words[a].rearrange("p t i -> p (t i)").bitcast(I32))
+
+        load_w(("e", 0, 0))
+        for r in range(4):
+            for a in range(2):
+                nc.sync.dma_start(out=tabs_t[4 * a + r : P : 32, :], in_=tab_scales[a, r:16:4, :].bitcast(I32))
+        nc.sync.dma_start(out=offs_t[:], in_=offs)
+        load_tab(0)
+        load_w(("e", 1, 0))
+        load_tab(1)
+        load_w(("o", 0, 0))
+        load_w(("o", 1, 0), SPLIT_LAST)
+        nc.sync.dma_start(out=pos1_t[:], in_=pos1)
+        nc.sync.dma_start(out=pos2_t[:], in_=pos2)
+        for key in (("e", 0, 1), ("e", 1, 1), ("o", 0, 1), ("o", 1, 1)):
+            load_w(key)
+        nc.sync.dma_start(
+            out=w2_t[:].bitcast(I32), in_=w2_words.rearrange("a p c -> p a c").bitcast(I32)
+        )
+        for q in range(4):
+            nc.sync.dma_start(
+                out=w2s_t[32 * q : 32 * q + 4, :, :].bitcast(I32),
+                in_=w2_scales[:, 4 * q : 4 * q + 4, :].rearrange("a r n -> r a n").bitcast(I32),
+            )
+
+        grouped = {}
+
+        def cast(key, parts=1):
+            g = ring.tile([P, PACK, P, PACK], BF16, name="grouped", tag="grouped", bufs=4, align_bytes=64)
+            grouped[key] = g
+            rows = P // parts
+            for h in range(parts):
+                dst = g[:, :, h * rows : (h + 1) * rows, :].rearrange("p t m j -> p m j t")
+                src = raw[key][:, :, h * rows * PACK : (h + 1) * rows * PACK].rearrange("p j (m t) -> p m j t", t=PACK)
+                eng = CAST_ON[key[0] + str(key[1]) + str(key[2])][h]
+                if eng == "v":
+                    nc.vector.tensor_copy(out=dst, in_=src)
+                elif eng == "s":
+                    nc.scalar.copy(out=dst, in_=src)
+                else:
+                    nc.gpsimd.tensor_scalar(out=dst, in0=src, scalar1=1.0, scalar2=0.0, op0=ALU.mult, op1=ALU.add)
+
+        def quant_w(key, parts=1):
+            flat = grouped[key][:].rearrange("p t m j -> p (t m j)")
+            w = KP // parts
+            for h in range(parts):
+                nc.vector.quantize_mx(
+                    out=codes[key][:, h * w : (h + 1) * w].bitcast(FP8X4),
+                    scales=scales[key][:, h * w : (h + 1) * w],
+                    in_=flat[:, h * w * PACK : (h + 1) * w * PACK],
+                )
+
+        def gather_tab(a, half):
+            cols = slice(half * BANK, (half + 1) * BANK)
+            lst = offs_t[:, half * BANK // 16 : (half + 1) * BANK // 16]
+            nc.vector.tensor_copy(out=v_t[a][:, cols], in_=tab_t[a][:].bitcast(U32).indirect(lst))
+
+        def square(m, b, t):
+            sq = ring.tile([P, S], F32, name="sq" + m, tag="sq" + m, bufs=5 if m == "e" else 4)
+            for half in range(2):
+                cols = slice(half * BANK, (half + 1) * BANK)
+                acc = psum.tile([P, BANK], F32, name="acc", tag="acc")
+                for a in range(2):
+                    nc.tensor.matmul_mx(
+                        out=acc[:],
+                        lhsT=codes[(m, a, b)][:, t * P : (t + 1) * P].bitcast(FP8X4),
+                        lhsT_scale=scales[(m, a, b)][:, t * P : (t + 1) * P],
+                        rhs=v_t[a][:, cols].bitcast(FP8X4),
+                        rhs_scale=vs_t[4 * a : P, cols],
+                        start=(a == 0),
+                        stop=(a == 1),
+                    )
+                nc.scalar.activation(out=sq[:, cols], in_=acc[:], func=ACT.Square, bias=bias0[:])
+            return sq
+
+        def amplitude(sq_e, sq_o, idx, parts):
+            ss = sq_o
+            h = ring.tile([P, S], F32, name="h", tag="h", bufs=3)
+            w = S // parts
+            for c in range(parts):
+                cols = slice(c * w, (c + 1) * w)
+                eng = nc.vector if ADD_ON[idx][c % len(ADD_ON[idx])] == "v" else nc.gpsimd
+                eng.tensor_tensor(out=ss[:, cols], in0=sq_e[:, cols], in1=sq_o[:, cols], op=ALU.add)
+                nc.scalar.activation(out=h[:, cols], in_=ss[:, cols], func=ACT.Sqrt)
+            return h
+
+        def pick(h, dst, t, lst, lo, hi):
+            nc.vector.tensor_copy(out=dst[:, t, lo:hi], in_=h[:].indirect(lst[:, lo // 16 : hi // 16]))
+
+        def difference(ha, hb, b, lo, hi):
+            z = ring.tile([P, (hi - lo) * PACK], BF16, name="z", tag="z%d" % b, bufs=1 + b, align_bytes=64)
+            eng = nc.vector if SUB_ON[b] == "v" else nc.gpsimd
+            eng.tensor_tensor(
+                out=z[:].rearrange("p (c i t) -> p c t i", i=4, t=PACK),
+                in0=ha[:, :, lo:hi].rearrange("p t (c i) -> p c t i", i=4),
+                in1=hb[:, :, lo:hi].rearrange("p t (c i) -> p c t i", i=4),
+                op=ALU.subtract,
+            )
+            return z
+
+        def quant_z(z, b, lo, hi):
+            nc.vector.quantize_mx(
+                out=z_codes[b][:, lo:hi].bitcast(FP8X4), scales=z_scales[b][:, lo:hi], in_=z[:]
+            )
+
+        out_v = out.rearrange("(g p) i -> p g i", p=P)
+
+        def readout(lo, hi):
+            res = ring.tile([P, N // P, hi - lo], F32, name="res", tag="res", bufs=4)
+            for c0 in range(lo, hi, P):
+                acc = psum.tile([P, N // P, P], F32, name="acc", tag="acc")
+                for g in range(N // P):
+                    for a in range(2):
+                        nc.tensor.matmul_mx(
+                            out=acc[:, g, :],
+                            lhsT=w2_t[:, a, 2 * g * P : 2 * (g + 1) * P].bitcast(FP4X4),
+                            lhsT_scale=w2s_t[:, a, g * P : (g + 1) * P],
+                            rhs=z_codes[a][:, c0 : c0 + P].bitcast(FP8X4),
+                            rhs_scale=z_scales[a][:, c0 : c0 + P],
+                            start=(a == 0),
+                            stop=(a == 1),
+                        )
+                nc.scalar.copy(out=res[:, :, c0 - lo : c0 - lo + P], in_=acc[:])
+            nc.sync.dma_start(out=out_v[:, :, lo:hi], in_=res[:])
+
+        cast(("e", 0, 0))
+        nc.vector.tensor_copy(out=vs_t[:], in_=tabs_t[:].bitcast(U8).indirect(offs_t[:]))
+        gather_tab(0, 0)
+        gather_tab(0, 1)
+        quant_w(("e", 0, 0))
+        cast(("e", 1, 0))
+        quant_w(("e", 1, 0))
+        gather_tab(1, 0)
+        gather_tab(1, 1)
+        sq_e = [square("e", 0, t) for t in range(PACK)]
+        cast(("o", 0, 0))
+        quant_w(("o", 0, 0))
+        cast(("o", 1, 0), SPLIT_LAST)
+        quant_w(("o", 1, 0), 4)
+
+        picks = [[keep.tile([P, PACK, NPAIR], F32, name="pick%d%d" % (b, u)) for u in range(2)] for b in range(2)]
+        later = [("e", 0, 1), ("e", 1, 1), ("o", 0, 1), ("o", 1, 1)]
+        for t in range(PACK):
+            h = amplitude(sq_e[t], square("o", 0, t), t, 2 if t == 0 or "g" in ADD_ON[t] else 1)
+            pick(h, picks[0][0], t, pos1_t, 0, NPAIR)
+            pick(h, picks[0][1], t, pos2_t, 0, NPAIR)
+            cast(later[t])
+            quant_w(later[t])
+        for t in range(PACK):
+            e2 = square("e", 1, t)
+            h = amplitude(e2, square("o", 1, t), 4 + t, 2 if "g" in ADD_ON[4 + t] else 1)
+            if t == 0:
+                quant_z(difference(picks[0][0], picks[0][1], 0, 0, NPAIR), 0, 0, NPAIR)
+            if t < PACK - 1:
+                pick(h, picks[1][0], t, pos1_t, 0, NPAIR)
+                pick(h, picks[1][1], t, pos2_t, 0, NPAIR)
+        w = NPAIR // TAIL
+        for c in range(TAIL):
+            lo, hi = c * w, (c + 1) * w
+            pick(h, picks[1][0], PACK - 1, pos1_t, lo, hi)
+            pick(h, picks[1][1], PACK - 1, pos2_t, lo, hi)
+            quant_z(difference(picks[1][0], picks[1][1], 1, lo, hi), 1, lo, hi)
+            readout(lo, hi)

@@ -1,6 +1,7 @@
 from contextlib import ExitStack
 
 import concourse.mybir as mybir
+from concourse.masks import make_identity
 
 K, T, S, NPAIR, H, N = 1024, 4096, 1024, 512, 1024, 512
 FLOPS = 2 * 2 * K * H * S + 2 * H * N * NPAIR
@@ -20,11 +21,14 @@ P = 128
 PACK = 4
 KP = P * PACK
 BANK = 512
-CAST_ON = {"e00": "s", "e10": "s", "o00": "v", "o10": "vv", "e01": "s", "e11": "s", "o01": "s", "o11": "s"}
-ADD_ON = ["v"] * 8
-SUB_ON = "vv"
-TAIL = 4
-SPLIT_LAST = 2
+CFG = {"tail": 4, "cast": {"e00": "v", "e10": "s", "o00": "vv", "o10": "vv", "e01": "v", "e11": "vv", "o01": "v", "o11": "ssss"}, "add": ["v", "p", "p", "v", "p", "v", "p", "p"], "sub": "vv", "cpos": [7, 3, 3, 0], "qpos": [7, 3, 3, 2], "qparts": [1, 1, 1, 1], "zpos": 15, "zparts": 2, "lag": 1, "loads": ["e0", "s", "t0", "e1", "t1", "o0", "o1"], "lparts": {"o1": 2, "e1": 1, "e0": 1, "o0": 1}, "hq": {"o1": 2, "o0": 1, "e0": 1, "e1": 1}, "epre": 3, "mmb": 8, "plag": 1, "first": 1, "grp": {"e0": 1, "e1": 1, "o0": 1, "o1": 1}, "sqb": {"e1": 4, "o1": 4, "e2": 2, "o2": 2, "e4": 2, "o4": 1}, "weave": "", "rescopy": "ssss"}
+TAG2 = "acc" if CFG["mmb"] == 8 else "acc2"
+BUF2 = 8 if CFG["mmb"] == 8 else 8 - CFG["mmb"]
+CAST_ON = CFG["cast"]
+ADD_ON = CFG["add"]
+SUB_ON = CFG["sub"]
+TAIL = CFG["tail"]
+SPLIT_LAST = len(CFG["cast"]["o10"])
 
 
 def tile_list_quadrature_motion_readout_kernel(
@@ -58,6 +62,8 @@ def tile_list_quadrature_motion_readout_kernel(
         z_codes = [keep.tile([P, NPAIR], U32, name="zc%d" % b, align_bytes=64) for b in range(2)]
         z_scales = [keep.tile([P, NPAIR], U8, name="zs%d" % b, align_bytes=64) for b in range(2)]
 
+        ident = keep.tile([P, P], F32, name="ident")
+        make_identity(nc, ident[:])
         nc.vector.memset(tabs_t[:], 0)
         nc.vector.memset(zero[:], 0.0)
         nc.vector.memset(w2s_t[:].rearrange("p a n -> p (a n)").bitcast(I32), 0)
@@ -66,7 +72,7 @@ def tile_list_quadrature_motion_readout_kernel(
         def load_w(key, parts=1):
             m, a, b = key
             width = KP // parts
-            raw[key] = ring.tile([P, PACK, KP], F32, name="raw", tag="raw", bufs=6, align_bytes=64)
+            raw[key] = ring.tile([P, PACK, KP], F32, name="raw", tag="raw", bufs=8, align_bytes=64)
             for h in range(parts):
                 src = w_in[m][a * KP : (a + 1) * KP, b * KP + h * width : b * KP + (h + 1) * width]
                 nc.sync.dma_start(
@@ -77,16 +83,16 @@ def tile_list_quadrature_motion_readout_kernel(
         def load_tab(a):
             nc.sync.dma_start(out=tab_t[a][:], in_=tab_words[a].rearrange("p t i -> p (t i)").bitcast(I32))
 
-        load_w(("e", 0, 0))
-        for r in range(4):
-            for a in range(2):
-                nc.sync.dma_start(out=tabs_t[4 * a + r : P : 32, :], in_=tab_scales[a, r:16:4, :].bitcast(I32))
-        nc.sync.dma_start(out=offs_t[:], in_=offs)
-        load_tab(0)
-        load_w(("e", 1, 0))
-        load_tab(1)
-        load_w(("o", 0, 0))
-        load_w(("o", 1, 0), SPLIT_LAST)
+        for item in CFG["loads"]:
+            if item == "s":
+                for r in range(4):
+                    for a in range(2):
+                        nc.sync.dma_start(out=tabs_t[4 * a + r : P : 32, :], in_=tab_scales[a, r:16:4, :].bitcast(I32))
+                nc.sync.dma_start(out=offs_t[:], in_=offs)
+            elif item[0] == "t":
+                load_tab(int(item[1]))
+            else:
+                load_w((item[0], int(item[1]), 0), CFG["lparts"].get(item, 1))
         nc.sync.dma_start(out=pos1_t[:], in_=pos1)
         nc.sync.dma_start(out=pos2_t[:], in_=pos2)
         for key in (("e", 0, 1), ("e", 1, 1), ("o", 0, 1), ("o", 1, 1)):
@@ -102,7 +108,8 @@ def tile_list_quadrature_motion_readout_kernel(
 
         grouped = {}
 
-        def cast(key, parts=1):
+        def cast(key):
+            parts = len(CAST_ON[key[0] + str(key[1]) + str(key[2])])
             g = ring.tile([P, PACK, P, PACK], BF16, name="grouped", tag="grouped", bufs=4, align_bytes=64)
             grouped[key] = g
             rows = P // parts
@@ -132,11 +139,39 @@ def tile_list_quadrature_motion_readout_kernel(
             lst = offs_t[:, half * BANK // 16 : (half + 1) * BANK // 16]
             nc.vector.tensor_copy(out=v_t[a][:, cols], in_=tab_t[a][:].bitcast(U32).indirect(lst))
 
+        made = {}
+
         def square(m, b, t):
-            sq = ring.tile([P, S], F32, name="sq" + m, tag="sq" + m, bufs=5 if m == "e" else 4)
+            if ADD_ON[4 * b + t] == "p":
+                g = CFG["grp"][m + str(b)]
+                while g > 1 and not all(ADD_ON[4 * b + u] == "p" for u in range(t // g * g, t // g * g + g)):
+                    g //= 2
+                t0 = t // g * g
+                if (m, b, t0) not in made:
+                    width = g * P
+                    sq = ring.tile([P, S // P, width], F32, name="sq" + m, tag="sq%s%d" % (m, g), bufs=CFG["sqb"][m + str(g)])
+                    per = BANK // width
+                    for j0 in range(0, S // P, per):
+                        acc = psum.tile([P, per, width], F32, name="acc", tag="acc", bufs=CFG["mmb"])
+                        for jj in range(per):
+                            js = slice((j0 + jj) * P, (j0 + jj + 1) * P)
+                            for a in range(2):
+                                nc.tensor.matmul_mx(
+                                    out=acc[:, jj, :],
+                                    lhsT=v_t[a][:, js].bitcast(FP8X4),
+                                    lhsT_scale=vs_t[4 * a : P, js],
+                                    rhs=codes[(m, a, b)][:, t0 * P : t0 * P + width].bitcast(FP8X4),
+                                    rhs_scale=scales[(m, a, b)][:, t0 * P : t0 * P + width],
+                                    start=(a == 0),
+                                    stop=(a == 1),
+                                )
+                        nc.scalar.activation(out=sq[:, j0 : j0 + per, :], in_=acc[:], func=ACT.Square, bias=bias0[:])
+                    made[(m, b, t0)] = sq
+                return made[(m, b, t0)][:, :, (t - t0) * P : (t - t0 + 1) * P]
+            sq = ring.tile([P, S], F32, name="sq" + m, tag="sq%s1" % m, bufs=CFG["sqb"][m + "1"])
             for half in range(2):
                 cols = slice(half * BANK, (half + 1) * BANK)
-                acc = psum.tile([P, BANK], F32, name="acc", tag="acc")
+                acc = psum.tile([P, BANK], F32, name="acc", tag="acc", bufs=CFG["mmb"])
                 for a in range(2):
                     nc.tensor.matmul_mx(
                         out=acc[:],
@@ -153,11 +188,24 @@ def tile_list_quadrature_motion_readout_kernel(
         def amplitude(sq_e, sq_o, idx, parts):
             ss = sq_o
             h = ring.tile([P, S], F32, name="h", tag="h", bufs=3)
+            if ADD_ON[idx] == "p":
+                for half in range(2):
+                    acc = psum.tile([P, BANK], F32, name="acc", tag=TAG2, bufs=BUF2)
+                    for j0 in range(0, BANK, P):
+                        jt = (half * BANK + j0) // P
+                        nc.tensor.matmul(acc[:, j0 : j0 + P], sq_e[:, jt, :], ident[:], start=True, stop=False, is_transpose=True)
+                        nc.tensor.matmul(acc[:, j0 : j0 + P], sq_o[:, jt, :], ident[:], start=False, stop=True, is_transpose=True)
+                    nc.scalar.activation(out=h[:, half * BANK : (half + 1) * BANK], in_=acc[:], func=ACT.Sqrt)
+                return h
             w = S // parts
             for c in range(parts):
                 cols = slice(c * w, (c + 1) * w)
-                eng = nc.vector if ADD_ON[idx][c % len(ADD_ON[idx])] == "v" else nc.gpsimd
-                eng.tensor_tensor(out=ss[:, cols], in0=sq_e[:, cols], in1=sq_o[:, cols], op=ALU.add)
+                if ADD_ON[idx][c % len(ADD_ON[idx])] == "v":
+                    nc.vector.tensor_tensor(out=ss[:, cols], in0=sq_e[:, cols], in1=sq_o[:, cols], op=ALU.add)
+                else:
+                    for c0 in range(c * w, (c + 1) * w, 256):
+                        piece = slice(c0, c0 + 256)
+                        nc.gpsimd.tensor_tensor(out=ss[:, piece], in0=sq_e[:, piece], in1=sq_o[:, piece], op=ALU.add)
                 nc.scalar.activation(out=h[:, cols], in_=ss[:, cols], func=ACT.Sqrt)
             return h
 
@@ -165,7 +213,7 @@ def tile_list_quadrature_motion_readout_kernel(
             nc.vector.tensor_copy(out=dst[:, t, lo:hi], in_=h[:].indirect(lst[:, lo // 16 : hi // 16]))
 
         def difference(ha, hb, b, lo, hi):
-            z = ring.tile([P, (hi - lo) * PACK], BF16, name="z", tag="z%d" % b, bufs=1 + b, align_bytes=64)
+            z = ring.tile([P, (hi - lo) * PACK], BF16, name="z", tag="z%d" % b, bufs=2, align_bytes=64)
             eng = nc.vector if SUB_ON[b] == "v" else nc.gpsimd
             eng.tensor_tensor(
                 out=z[:].rearrange("p (c i t) -> p c t i", i=4, t=PACK),
@@ -175,6 +223,19 @@ def tile_list_quadrature_motion_readout_kernel(
             )
             return z
 
+        def diff_rows(ha, hb, t, lo, hi):
+            nc.vector.tensor_tensor(out=ha[:, t, lo:hi], in0=ha[:, t, lo:hi], in1=hb[:, t, lo:hi], op=ALU.subtract)
+
+        def weave(ha, b, lo, hi, eng):
+            z = ring.tile([P, (hi - lo) * PACK], BF16, name="z", tag="z%d" % b, bufs=2, align_bytes=64)
+            dst = z[:].rearrange("p (c i t) -> p c t i", i=4, t=PACK)
+            src = ha[:, :, lo:hi].rearrange("p t (c i) -> p c t i", i=4)
+            if eng == "s":
+                nc.scalar.copy(out=dst, in_=src)
+            else:
+                nc.vector.tensor_copy(out=dst, in_=src)
+            return z
+
         def quant_z(z, b, lo, hi):
             nc.vector.quantize_mx(
                 out=z_codes[b][:, lo:hi].bitcast(FP8X4), scales=z_scales[b][:, lo:hi], in_=z[:]
@@ -182,10 +243,10 @@ def tile_list_quadrature_motion_readout_kernel(
 
         out_v = out.rearrange("(g p) i -> p g i", p=P)
 
-        def readout(lo, hi):
+        def readout(lo, hi, eng):
             res = ring.tile([P, N // P, hi - lo], F32, name="res", tag="res", bufs=4)
             for c0 in range(lo, hi, P):
-                acc = psum.tile([P, N // P, P], F32, name="acc", tag="acc")
+                acc = psum.tile([P, N // P, P], F32, name="acc", tag=TAG2, bufs=BUF2)
                 for g in range(N // P):
                     for a in range(2):
                         nc.tensor.matmul_mx(
@@ -197,44 +258,66 @@ def tile_list_quadrature_motion_readout_kernel(
                             start=(a == 0),
                             stop=(a == 1),
                         )
-                nc.scalar.copy(out=res[:, :, c0 - lo : c0 - lo + P], in_=acc[:])
+                if eng == "s":
+                    nc.scalar.copy(out=res[:, :, c0 - lo : c0 - lo + P], in_=acc[:])
+                else:
+                    nc.vector.tensor_copy(out=res[:, :, c0 - lo : c0 - lo + P], in_=acc[:])
             nc.sync.dma_start(out=out_v[:, :, lo:hi], in_=res[:])
 
-        cast(("e", 0, 0))
-        nc.vector.tensor_copy(out=vs_t[:], in_=tabs_t[:].bitcast(U8).indirect(offs_t[:]))
-        gather_tab(0, 0)
-        gather_tab(0, 1)
-        quant_w(("e", 0, 0))
-        cast(("e", 1, 0))
-        quant_w(("e", 1, 0))
-        gather_tab(1, 0)
-        gather_tab(1, 1)
-        sq_e = [square("e", 0, t) for t in range(PACK)]
-        cast(("o", 0, 0))
-        quant_w(("o", 0, 0))
-        cast(("o", 1, 0), SPLIT_LAST)
-        quant_w(("o", 1, 0), 4)
+        for item in CFG["loads"]:
+            if item == "s":
+                nc.vector.tensor_copy(out=vs_t[:], in_=tabs_t[:].bitcast(U8).indirect(offs_t[:]))
+            elif item[0] == "t":
+                gather_tab(int(item[1]), 0)
+                gather_tab(int(item[1]), 1)
+            else:
+                cast((item[0], int(item[1]), 0))
+                quant_w((item[0], int(item[1]), 0), CFG["hq"].get(item, 1))
+        sq_e = [square("e", 0, t) for t in range(CFG["epre"])]
 
-        picks = [[keep.tile([P, PACK, NPAIR], F32, name="pick%d%d" % (b, u)) for u in range(2)] for b in range(2)]
+        picks = [[ring.tile([P, PACK, NPAIR], F32, name="pick%d%d" % (b, u), tag="raw", bufs=8, align_bytes=64) for u in range(2)] for b in range(2)]
         later = [("e", 0, 1), ("e", 1, 1), ("o", 0, 1), ("o", 1, 1)]
-        for t in range(PACK):
-            h = amplitude(sq_e[t], square("o", 0, t), t, 2 if t == 0 or "g" in ADD_ON[t] else 1)
-            pick(h, picks[0][0], t, pos1_t, 0, NPAIR)
-            pick(h, picks[0][1], t, pos2_t, 0, NPAIR)
-            cast(later[t])
-            quant_w(later[t])
-        for t in range(PACK):
-            e2 = square("e", 1, t)
-            h = amplitude(e2, square("o", 1, t), 4 + t, 2 if "g" in ADD_ON[4 + t] else 1)
-            if t == 0:
-                quant_z(difference(picks[0][0], picks[0][1], 0, 0, NPAIR), 0, 0, NPAIR)
-            if t < PACK - 1:
-                pick(h, picks[1][0], t, pos1_t, 0, NPAIR)
-                pick(h, picks[1][1], t, pos2_t, 0, NPAIR)
+        def extras(pos):
+            for i, key in enumerate(later):
+                if CFG["cpos"][i] == pos:
+                    cast(key)
+            for i, key in enumerate(later):
+                if CFG["qpos"][i] == pos:
+                    quant_w(key, CFG["qparts"][i])
+            if CFG["zpos"] == pos:
+                for c in range(CFG["zparts"]):
+                    lo, hi = c * NPAIR // CFG["zparts"], (c + 1) * NPAIR // CFG["zparts"]
+                    quant_z(difference(picks[0][0], picks[0][1], 0, lo, hi), 0, lo, hi)
+
+        hs = {}
+        sqs = {}
+        for step in range(2 * PACK + CFG["plag"] + CFG["lag"]):
+            if step < 2 * PACK:
+                b, t = divmod(step, PACK)
+                e2 = sq_e[t] if step < CFG["epre"] else square("e", b, t)
+                sqs[step] = (e2, square("o", b, t))
+            v = step - CFG["plag"]
+            if step == 0 and CFG["first"]:
+                v = 0
+            if 0 <= v < 2 * PACK and v not in hs:
+                hs[v] = amplitude(sqs[v][0], sqs[v][1], v, 2 if v == 0 or "g" in ADD_ON[v] else 1)
+            extras(2 * step)
+            u = step - CFG["lag"] - CFG["plag"]
+            if 0 <= u < 2 * PACK - 1:
+                pick(hs[u], picks[u // PACK][0], u % PACK, pos1_t, 0, NPAIR)
+                pick(hs[u], picks[u // PACK][1], u % PACK, pos2_t, 0, NPAIR)
+                if u >= PACK and CFG["weave"]:
+                    diff_rows(picks[1][0], picks[1][1], u % PACK, 0, NPAIR)
+            extras(2 * step + 1)
+        h = hs[2 * PACK - 1]
         w = NPAIR // TAIL
         for c in range(TAIL):
             lo, hi = c * w, (c + 1) * w
             pick(h, picks[1][0], PACK - 1, pos1_t, lo, hi)
             pick(h, picks[1][1], PACK - 1, pos2_t, lo, hi)
-            quant_z(difference(picks[1][0], picks[1][1], 1, lo, hi), 1, lo, hi)
-            readout(lo, hi)
+            if CFG["weave"]:
+                diff_rows(picks[1][0], picks[1][1], PACK - 1, lo, hi)
+                quant_z(weave(picks[1][0], 1, lo, hi, CFG["weave"][c]), 1, lo, hi)
+            else:
+                quant_z(difference(picks[1][0], picks[1][1], 1, lo, hi), 1, lo, hi)
+            readout(lo, hi, CFG["rescopy"][c])

@@ -21,14 +21,13 @@ P = 128
 PACK = 4
 KP = P * PACK
 BANK = 512
-CFG = {"tail": 4, "cast": {"e00": "v", "e10": "s", "o00": "vv", "o10": "vv", "e01": "v", "e11": "vv", "o01": "v", "o11": "ssss"}, "add": ["v", "p", "p", "v", "p", "v", "p", "p"], "sub": "vv", "cpos": [7, 3, 3, 0], "qpos": [7, 3, 3, 2], "qparts": [1, 1, 1, 1], "zpos": 15, "zparts": 2, "lag": 1, "loads": ["e0", "s", "t0", "e1", "t1", "o0", "o1"], "lparts": {"o1": 2, "e1": 1, "e0": 1, "o0": 1}, "hq": {"o1": 2, "o0": 1, "e0": 1, "e1": 1}, "epre": 3, "mmb": 8, "plag": 1, "first": 1, "grp": {"e0": 1, "e1": 1, "o0": 1, "o1": 1}, "sqb": {"e1": 4, "o1": 4, "e2": 2, "o2": 2, "e4": 2, "o4": 1}, "weave": "", "rescopy": "ssss"}
+CFG = {"tail": 4, "cast": {"e00": "v", "e10": "v", "o00": "v", "o10": "vv", "e01": "v", "e11": "v", "o01": "ssss", "o11": "v"}, "add": ["v", "p", "p", "p", "p", "p", "v", "p"], "sub": "vv", "loads": ["s", "e1", "f", "t0", "l", "e0", "u", "t1", "o0", "o1"], "lparts": {"o1": 2}, "qp": {"o10": 4, "o00": 4, "o11": 2, "o01": 2}, "mmb": 8, "grp": {"e0": 1, "e1": 2, "o0": 1, "o1": 1}, "sqb": {"e1": 4, "o1": 3, "e2": 2, "o2": 1, "e4": 1, "o4": 1}, "weave": "", "rescopy": "ssss", "pre": 1, "st2": 0, "ap": [2, 1, 1, 1, 1, 1, 2, 1], "rawb": 4, "grpb": 3, "hb": 3, "order": ["ce10", "qe10", "t00", "t01", "ce00", "qe00", "s", "t10", "t11", "co00", "qo00", "co10", "qo10", "E0", "E1", "E2", "O0", "A0", "ce01", "qe01", "O1", "ce11", "qe11", "E3", "O2", "A1", "co01", "co11", "qo01", "qo11", "O3", "A2", "G0", "H0", "E4", "A3", "G1", "H1", "E5", "O4", "G2", "H2", "E6", "O5", "A4", "G3", "H3", "E7", "A5", "Z0", "Z1", "Y0", "Y1", "O6", "O7", "G4", "H4", "A6", "A7", "G5", "H5", "G6", "H6"]}
 TAG2 = "acc" if CFG["mmb"] == 8 else "acc2"
 BUF2 = 8 if CFG["mmb"] == 8 else 8 - CFG["mmb"]
 CAST_ON = CFG["cast"]
 ADD_ON = CFG["add"]
 SUB_ON = CFG["sub"]
 TAIL = CFG["tail"]
-SPLIT_LAST = len(CFG["cast"]["o10"])
 
 
 def tile_list_quadrature_motion_readout_kernel(
@@ -67,12 +66,11 @@ def tile_list_quadrature_motion_readout_kernel(
         nc.vector.memset(tabs_t[:], 0)
         nc.vector.memset(zero[:], 0.0)
         nc.vector.memset(w2s_t[:].rearrange("p a n -> p (a n)").bitcast(I32), 0)
-        nc.scalar.activation(out=bias0[:], in_=zero[:], func=ACT.Sqrt)
 
         def load_w(key, parts=1):
             m, a, b = key
             width = KP // parts
-            raw[key] = ring.tile([P, PACK, KP], F32, name="raw", tag="raw", bufs=8, align_bytes=64)
+            raw[key] = ring.tile([P, PACK, KP], F32, name="raw", tag="raw", bufs=CFG["rawb"], align_bytes=64)
             for h in range(parts):
                 src = w_in[m][a * KP : (a + 1) * KP, b * KP + h * width : b * KP + (h + 1) * width]
                 nc.sync.dma_start(
@@ -84,17 +82,19 @@ def tile_list_quadrature_motion_readout_kernel(
             nc.sync.dma_start(out=tab_t[a][:], in_=tab_words[a].rearrange("p t i -> p (t i)").bitcast(I32))
 
         for item in CFG["loads"]:
-            if item == "s":
-                for r in range(4):
+            if item in "su":
+                for r in ((0, 1) if item == "s" else (2, 3)):
                     for a in range(2):
                         nc.sync.dma_start(out=tabs_t[4 * a + r : P : 32, :], in_=tab_scales[a, r:16:4, :].bitcast(I32))
+            elif item == "f":
                 nc.sync.dma_start(out=offs_t[:], in_=offs)
+            elif item == "l":
+                nc.sync.dma_start(out=pos1_t[:], in_=pos1)
+                nc.sync.dma_start(out=pos2_t[:], in_=pos2)
             elif item[0] == "t":
                 load_tab(int(item[1]))
             else:
                 load_w((item[0], int(item[1]), 0), CFG["lparts"].get(item, 1))
-        nc.sync.dma_start(out=pos1_t[:], in_=pos1)
-        nc.sync.dma_start(out=pos2_t[:], in_=pos2)
         for key in (("e", 0, 1), ("e", 1, 1), ("o", 0, 1), ("o", 1, 1)):
             load_w(key)
         nc.sync.dma_start(
@@ -106,11 +106,13 @@ def tile_list_quadrature_motion_readout_kernel(
                 in_=w2_scales[:, 4 * q : 4 * q + 4, :].rearrange("a r n -> r a n").bitcast(I32),
             )
 
+        nc.scalar.activation(out=bias0[:], in_=zero[:], func=ACT.Sqrt)
         grouped = {}
+        zs0 = {}
 
         def cast(key):
             parts = len(CAST_ON[key[0] + str(key[1]) + str(key[2])])
-            g = ring.tile([P, PACK, P, PACK], BF16, name="grouped", tag="grouped", bufs=4, align_bytes=64)
+            g = ring.tile([P, PACK, P, PACK], BF16, name="grouped", tag="grouped", bufs=CFG["grpb"], align_bytes=64)
             grouped[key] = g
             rows = P // parts
             for h in range(parts):
@@ -187,7 +189,7 @@ def tile_list_quadrature_motion_readout_kernel(
 
         def amplitude(sq_e, sq_o, idx, parts):
             ss = sq_o
-            h = ring.tile([P, S], F32, name="h", tag="h", bufs=3)
+            h = ring.tile([P, S], F32, name="h", tag="h", bufs=CFG["hb"])
             if ADD_ON[idx] == "p":
                 for half in range(2):
                     acc = psum.tile([P, BANK], F32, name="acc", tag=TAG2, bufs=BUF2)
@@ -243,6 +245,30 @@ def tile_list_quadrature_motion_readout_kernel(
 
         out_v = out.rearrange("(g p) i -> p g i", p=P)
 
+        def w2_pass(acc, g, a, c0):
+            nc.tensor.matmul_mx(
+                out=acc,
+                lhsT=w2_t[:, a, 2 * g * P : 2 * (g + 1) * P].bitcast(FP4X4),
+                lhsT_scale=w2s_t[:, a, g * P : (g + 1) * P],
+                rhs=z_codes[a][:, c0 : c0 + P].bitcast(FP8X4),
+                rhs_scale=z_scales[a][:, c0 : c0 + P],
+                start=(a == 0),
+                stop=(a == 1),
+            )
+
+        def readout_split(lo, accs):
+            res = ring.tile([P, N // P, P], F32, name="res", tag="res", bufs=4)
+            for g in range(N // P):
+                w2_pass(accs[g][:], g, 1, lo)
+                if g % 2 == 0:
+                    nc.scalar.copy(out=res[:, g, :], in_=accs[g][:])
+                else:
+                    nc.vector.tensor_copy(out=res[:, g, :], in_=accs[g][:])
+                if CFG["st2"] and g % 2 == 1:
+                    nc.sync.dma_start(out=out_v[:, g - 1 : g + 1, lo : lo + P], in_=res[:, g - 1 : g + 1, :])
+            if not CFG["st2"]:
+                nc.sync.dma_start(out=out_v[:, :, lo : lo + P], in_=res[:])
+
         def readout(lo, hi, eng):
             res = ring.tile([P, N // P, hi - lo], F32, name="res", tag="res", bufs=4)
             for c0 in range(lo, hi, P):
@@ -264,51 +290,40 @@ def tile_list_quadrature_motion_readout_kernel(
                     nc.vector.tensor_copy(out=res[:, :, c0 - lo : c0 - lo + P], in_=acc[:])
             nc.sync.dma_start(out=out_v[:, :, lo:hi], in_=res[:])
 
-        for item in CFG["loads"]:
-            if item == "s":
-                nc.vector.tensor_copy(out=vs_t[:], in_=tabs_t[:].bitcast(U8).indirect(offs_t[:]))
-            elif item[0] == "t":
-                gather_tab(int(item[1]), 0)
-                gather_tab(int(item[1]), 1)
-            else:
-                cast((item[0], int(item[1]), 0))
-                quant_w((item[0], int(item[1]), 0), CFG["hq"].get(item, 1))
-        sq_e = [square("e", 0, t) for t in range(CFG["epre"])]
-
-        picks = [[ring.tile([P, PACK, NPAIR], F32, name="pick%d%d" % (b, u), tag="raw", bufs=8, align_bytes=64) for u in range(2)] for b in range(2)]
-        later = [("e", 0, 1), ("e", 1, 1), ("o", 0, 1), ("o", 1, 1)]
-        def extras(pos):
-            for i, key in enumerate(later):
-                if CFG["cpos"][i] == pos:
-                    cast(key)
-            for i, key in enumerate(later):
-                if CFG["qpos"][i] == pos:
-                    quant_w(key, CFG["qparts"][i])
-            if CFG["zpos"] == pos:
-                for c in range(CFG["zparts"]):
-                    lo, hi = c * NPAIR // CFG["zparts"], (c + 1) * NPAIR // CFG["zparts"]
-                    quant_z(difference(picks[0][0], picks[0][1], 0, lo, hi), 0, lo, hi)
-
+        picks = {}
         hs = {}
         sqs = {}
-        for step in range(2 * PACK + CFG["plag"] + CFG["lag"]):
-            if step < 2 * PACK:
-                b, t = divmod(step, PACK)
-                e2 = sq_e[t] if step < CFG["epre"] else square("e", b, t)
-                sqs[step] = (e2, square("o", b, t))
-            v = step - CFG["plag"]
-            if step == 0 and CFG["first"]:
-                v = 0
-            if 0 <= v < 2 * PACK and v not in hs:
-                hs[v] = amplitude(sqs[v][0], sqs[v][1], v, 2 if v == 0 or "g" in ADD_ON[v] else 1)
-            extras(2 * step)
-            u = step - CFG["lag"] - CFG["plag"]
-            if 0 <= u < 2 * PACK - 1:
-                pick(hs[u], picks[u // PACK][0], u % PACK, pos1_t, 0, NPAIR)
-                pick(hs[u], picks[u // PACK][1], u % PACK, pos2_t, 0, NPAIR)
-                if u >= PACK and CFG["weave"]:
-                    diff_rows(picks[1][0], picks[1][1], u % PACK, 0, NPAIR)
-            extras(2 * step + 1)
+        for tok in CFG["order"]:
+            kind = tok[0]
+            if kind == "c":
+                cast((tok[1], int(tok[2]), int(tok[3])))
+            elif kind == "q":
+                quant_w((tok[1], int(tok[2]), int(tok[3])), CFG["qp"].get(tok[1:], 1))
+            elif kind == "s":
+                nc.vector.tensor_copy(out=vs_t[:], in_=tabs_t[:].bitcast(U8).indirect(offs_t[:]))
+            elif kind == "t":
+                gather_tab(int(tok[1]), int(tok[2]))
+            elif kind in "EO":
+                u = int(tok[1])
+                sqs[tok] = square("e" if kind == "E" else "o", u // PACK, u % PACK)
+            elif kind == "A":
+                u = int(tok[1])
+                hs[u] = amplitude(sqs["E%d" % u], sqs["O%d" % u], u, CFG["ap"][u])
+            elif kind in "GH":
+                u = int(tok[1])
+                side = 0 if kind == "G" else 1
+                key = (u // PACK, side)
+                if key not in picks:
+                    picks[key] = ring.tile([P, PACK, NPAIR], F32, name="pick%d%d" % key, tag="pick", bufs=4, align_bytes=64)
+                pick(hs[u], picks[key], u % PACK, (pos1_t, pos2_t)[side], 0, NPAIR)
+            else:
+                c = int(tok[1])
+                lo, hi = c * NPAIR // 2, (c + 1) * NPAIR // 2
+                if kind == "Z":
+                    zs0[c] = difference(picks[(0, 0)], picks[(0, 1)], 0, lo, hi)
+                else:
+                    quant_z(zs0[c], 0, lo, hi)
+        picks = [[picks[(b, u)] for u in range(2)] for b in range(2)]
         h = hs[2 * PACK - 1]
         w = NPAIR // TAIL
         for c in range(TAIL):
@@ -320,4 +335,11 @@ def tile_list_quadrature_motion_readout_kernel(
                 quant_z(weave(picks[1][0], 1, lo, hi, CFG["weave"][c]), 1, lo, hi)
             else:
                 quant_z(difference(picks[1][0], picks[1][1], 1, lo, hi), 1, lo, hi)
-            readout(lo, hi, CFG["rescopy"][c])
+            if c == TAIL - 2 and CFG["pre"]:
+                accs = [psum.tile([P, P], F32, name="acc", tag="acc", bufs=CFG["mmb"]) for g in range(N // P)]
+                for g in range(N // P):
+                    w2_pass(accs[g][:], g, 0, NPAIR - P)
+            if c == TAIL - 1 and CFG["pre"]:
+                readout_split(lo, accs)
+            else:
+                readout(lo, hi, CFG["rescopy"][c])

@@ -21,13 +21,10 @@ P = 128
 PACK = 4
 KP = P * PACK
 BANK = 512
-CFG = {"tail": 4, "cast": {"e00": "v", "e10": "v", "o00": "v", "o10": "vv", "e01": "v", "e11": "v", "o01": "ssss", "o11": "v"}, "add": ["v", "p", "p", "p", "p", "p", "v", "p"], "sub": "vv", "loads": ["s", "e1", "f", "t0", "l", "e0", "u", "t1", "o0", "o1"], "lparts": {"o1": 2}, "qp": {"o10": 4, "o00": 4, "o11": 2, "o01": 2}, "mmb": 8, "grp": {"e0": 1, "e1": 2, "o0": 1, "o1": 1}, "sqb": {"e1": 4, "o1": 3, "e2": 2, "o2": 1, "e4": 1, "o4": 1}, "weave": "", "rescopy": "ssss", "pre": 1, "st2": 0, "ap": [2, 1, 1, 1, 1, 1, 2, 1], "rawb": 4, "grpb": 3, "hb": 3, "order": ["ce10", "qe10", "t00", "t01", "ce00", "qe00", "s", "t10", "t11", "co00", "qo00", "co10", "qo10", "E0", "E1", "E2", "O0", "A0", "ce01", "qe01", "O1", "ce11", "qe11", "E3", "O2", "A1", "co01", "co11", "qo01", "qo11", "O3", "A2", "G0", "H0", "E4", "A3", "G1", "H1", "E5", "O4", "G2", "H2", "E6", "O5", "A4", "G3", "H3", "E7", "A5", "Z0", "Z1", "Y0", "Y1", "O6", "O7", "G4", "H4", "A6", "A7", "G5", "H5", "G6", "H6"]}
-TAG2 = "acc" if CFG["mmb"] == 8 else "acc2"
-BUF2 = 8 if CFG["mmb"] == 8 else 8 - CFG["mmb"]
-CAST_ON = CFG["cast"]
-ADD_ON = CFG["add"]
-SUB_ON = CFG["sub"]
-TAIL = CFG["tail"]
+RAW_BUFS = 4
+VEC_BUFS = 6
+SCA_BUFS = 12
+PIECES = 4
 
 
 def tile_list_quadrature_motion_readout_kernel(
@@ -51,74 +48,57 @@ def tile_list_quadrature_motion_readout_kernel(
         zero = keep.tile([P, 1], F32, name="zero")
         bias0 = keep.tile([P, 1], F32, name="bias0")
         w_in = {"e": we, "o": wo}
-        raw, codes, scales = {}, {}, {}
+        raw, codes, scales, grouped = {}, {}, {}, {}
         for m in "eo":
             for a in range(2):
                 for b in range(2):
-                    key = (m, a, b)
-                    codes[key] = keep.tile([P, KP], U32, name="wc%s%d%d" % key, align_bytes=64)
-                    scales[key] = keep.tile([P, KP], U8, name="ws%s%d%d" % key, align_bytes=64)
+                    key = "%s%d%d" % (m, a, b)
+                    codes[key] = keep.tile([P, KP], U32, name="wc" + key, align_bytes=64)
+                    scales[key] = keep.tile([P, KP], U8, name="ws" + key, align_bytes=64)
         z_codes = [keep.tile([P, NPAIR], U32, name="zc%d" % b, align_bytes=64) for b in range(2)]
         z_scales = [keep.tile([P, NPAIR], U8, name="zs%d" % b, align_bytes=64) for b in range(2)]
-
+        diff = [keep.tile([P, PACK, NPAIR], F32, name="diff%d" % b, align_bytes=64) for b in range(2)]
         ident = keep.tile([P, P], F32, name="ident")
-        make_identity(nc, ident[:])
-        nc.vector.memset(tabs_t[:], 0)
-        nc.vector.memset(zero[:], 0.0)
-        nc.vector.memset(w2s_t[:].rearrange("p a n -> p (a n)").bitcast(I32), 0)
+
+        def vec_tile(shape, dtype, name):
+            return ring.tile(shape, dtype, name=name, tag="vec", bufs=VEC_BUFS, align_bytes=64)
+
+        def sca_tile(shape, dtype, name):
+            return ring.tile(shape, dtype, name=name, tag="sca", bufs=SCA_BUFS, align_bytes=64)
+
+        def bank(shape):
+            return psum.tile(shape, F32, name="acc", tag="acc", bufs=8)
 
         def load_w(key, parts=1):
-            m, a, b = key
+            a, b = int(key[1]), int(key[2])
             width = KP // parts
-            raw[key] = ring.tile([P, PACK, KP], F32, name="raw", tag="raw", bufs=CFG["rawb"], align_bytes=64)
+            raw[key] = []
             for h in range(parts):
-                src = w_in[m][a * KP : (a + 1) * KP, b * KP + h * width : b * KP + (h + 1) * width]
-                nc.sync.dma_start(
-                    out=raw[key][:, :, h * width : (h + 1) * width],
-                    in_=src.rearrange("(p j) r -> p j r", j=PACK),
-                )
+                r = ring.tile([P, PACK, width], F32, name="raw" + key, tag="raw%d" % parts, bufs=RAW_BUFS if parts == 1 else parts, align_bytes=64)
+                src = w_in[key[0]][a * KP : (a + 1) * KP, b * KP + h * width : b * KP + (h + 1) * width]
+                nc.sync.dma_start(out=r[:], in_=src.rearrange("(p j) r -> p j r", j=PACK))
+                raw[key].append(r)
 
         def load_tab(a):
             nc.sync.dma_start(out=tab_t[a][:], in_=tab_words[a].rearrange("p t i -> p (t i)").bitcast(I32))
 
-        for item in CFG["loads"]:
-            if item in "su":
-                for r in ((0, 1) if item == "s" else (2, 3)):
-                    for a in range(2):
-                        nc.sync.dma_start(out=tabs_t[4 * a + r : P : 32, :], in_=tab_scales[a, r:16:4, :].bitcast(I32))
-            elif item == "f":
-                nc.sync.dma_start(out=offs_t[:], in_=offs)
-            elif item == "l":
-                nc.sync.dma_start(out=pos1_t[:], in_=pos1)
-                nc.sync.dma_start(out=pos2_t[:], in_=pos2)
-            elif item[0] == "t":
-                load_tab(int(item[1]))
-            else:
-                load_w((item[0], int(item[1]), 0), CFG["lparts"].get(item, 1))
-        for key in (("e", 0, 1), ("e", 1, 1), ("o", 0, 1), ("o", 1, 1)):
-            load_w(key)
-        nc.sync.dma_start(
-            out=w2_t[:].bitcast(I32), in_=w2_words.rearrange("a p c -> p a c").bitcast(I32)
-        )
-        for q in range(4):
-            nc.sync.dma_start(
-                out=w2s_t[32 * q : 32 * q + 4, :, :].bitcast(I32),
-                in_=w2_scales[:, 4 * q : 4 * q + 4, :].rearrange("a r n -> r a n").bitcast(I32),
-            )
+        def load_scales(rows):
+            for r in rows:
+                for a in range(2):
+                    nc.sync.dma_start(out=tabs_t[4 * a + r : P : 32, :], in_=tab_scales[a, r:16:4, :].bitcast(I32))
 
-        nc.scalar.activation(out=bias0[:], in_=zero[:], func=ACT.Sqrt)
-        grouped = {}
-        zs0 = {}
-
-        def cast(key):
-            parts = len(CAST_ON[key[0] + str(key[1]) + str(key[2])])
-            g = ring.tile([P, PACK, P, PACK], BF16, name="grouped", tag="grouped", bufs=CFG["grpb"], align_bytes=64)
+        def cast(key, engines):
+            make = sca_tile if engines[0] == "s" else vec_tile
+            g = make([P, PACK, P, PACK], BF16, "g" + key)
             grouped[key] = g
-            rows = P // parts
-            for h in range(parts):
-                dst = g[:, :, h * rows : (h + 1) * rows, :].rearrange("p t m j -> p m j t")
-                src = raw[key][:, :, h * rows * PACK : (h + 1) * rows * PACK].rearrange("p j (m t) -> p m j t", t=PACK)
-                eng = CAST_ON[key[0] + str(key[1]) + str(key[2])][h]
+            rows = P // len(engines)
+            per_load = P // len(raw[key])
+            for h, eng in enumerate(engines):
+                m0 = h * rows
+                r = raw[key][m0 // per_load]
+                c0 = (m0 % per_load) * PACK
+                dst = g[:, :, m0 : m0 + rows, :].rearrange("p t m j -> p m j t")
+                src = r[:, :, c0 : c0 + rows * PACK].rearrange("p j (m t) -> p m j t", t=PACK)
                 if eng == "v":
                     nc.vector.tensor_copy(out=dst, in_=src)
                 elif eng == "s":
@@ -126,122 +106,114 @@ def tile_list_quadrature_motion_readout_kernel(
                 else:
                     nc.gpsimd.tensor_scalar(out=dst, in0=src, scalar1=1.0, scalar2=0.0, op0=ALU.mult, op1=ALU.add)
 
-        def quant_w(key, parts=1):
+        def quant_w(key, t0=0, t1=PACK):
             flat = grouped[key][:].rearrange("p t m j -> p (t m j)")
-            w = KP // parts
-            for h in range(parts):
-                nc.vector.quantize_mx(
-                    out=codes[key][:, h * w : (h + 1) * w].bitcast(FP8X4),
-                    scales=scales[key][:, h * w : (h + 1) * w],
-                    in_=flat[:, h * w * PACK : (h + 1) * w * PACK],
-                )
+            nc.vector.quantize_mx(
+                out=codes[key][:, t0 * P : t1 * P].bitcast(FP8X4),
+                scales=scales[key][:, t0 * P : t1 * P],
+                in_=flat[:, t0 * KP : t1 * KP],
+            )
 
         def gather_tab(a, half):
             cols = slice(half * BANK, (half + 1) * BANK)
             lst = offs_t[:, half * BANK // 16 : (half + 1) * BANK // 16]
             nc.vector.tensor_copy(out=v_t[a][:, cols], in_=tab_t[a][:].bitcast(U32).indirect(lst))
 
-        made = {}
+        sq, hs = {}, {}
 
-        def square(m, b, t):
-            if ADD_ON[4 * b + t] == "p":
-                g = CFG["grp"][m + str(b)]
-                while g > 1 and not all(ADD_ON[4 * b + u] == "p" for u in range(t // g * g, t // g * g + g)):
-                    g //= 2
-                t0 = t // g * g
-                if (m, b, t0) not in made:
-                    width = g * P
-                    sq = ring.tile([P, S // P, width], F32, name="sq" + m, tag="sq%s%d" % (m, g), bufs=CFG["sqb"][m + str(g)])
-                    per = BANK // width
-                    for j0 in range(0, S // P, per):
-                        acc = psum.tile([P, per, width], F32, name="acc", tag="acc", bufs=CFG["mmb"])
-                        for jj in range(per):
-                            js = slice((j0 + jj) * P, (j0 + jj + 1) * P)
-                            for a in range(2):
-                                nc.tensor.matmul_mx(
-                                    out=acc[:, jj, :],
-                                    lhsT=v_t[a][:, js].bitcast(FP8X4),
-                                    lhsT_scale=vs_t[4 * a : P, js],
-                                    rhs=codes[(m, a, b)][:, t0 * P : t0 * P + width].bitcast(FP8X4),
-                                    rhs_scale=scales[(m, a, b)][:, t0 * P : t0 * P + width],
-                                    start=(a == 0),
-                                    stop=(a == 1),
-                                )
-                        nc.scalar.activation(out=sq[:, j0 : j0 + per, :], in_=acc[:], func=ACT.Square, bias=bias0[:])
-                    made[(m, b, t0)] = sq
-                return made[(m, b, t0)][:, :, (t - t0) * P : (t - t0 + 1) * P]
-            sq = ring.tile([P, S], F32, name="sq" + m, tag="sq%s1" % m, bufs=CFG["sqb"][m + "1"])
+        def square_rows(m, u):
+            b, t = divmod(u, PACK)
+            sq[(m, u)] = sca_tile([P, S], F32, "sq%s%d" % (m, u))
             for half in range(2):
                 cols = slice(half * BANK, (half + 1) * BANK)
-                acc = psum.tile([P, BANK], F32, name="acc", tag="acc", bufs=CFG["mmb"])
+                acc = bank([P, BANK])
                 for a in range(2):
+                    key = "%s%d%d" % (m, a, b)
                     nc.tensor.matmul_mx(
                         out=acc[:],
-                        lhsT=codes[(m, a, b)][:, t * P : (t + 1) * P].bitcast(FP8X4),
-                        lhsT_scale=scales[(m, a, b)][:, t * P : (t + 1) * P],
+                        lhsT=codes[key][:, t * P : (t + 1) * P].bitcast(FP8X4),
+                        lhsT_scale=scales[key][:, t * P : (t + 1) * P],
                         rhs=v_t[a][:, cols].bitcast(FP8X4),
                         rhs_scale=vs_t[4 * a : P, cols],
                         start=(a == 0),
                         stop=(a == 1),
                     )
-                nc.scalar.activation(out=sq[:, cols], in_=acc[:], func=ACT.Square, bias=bias0[:])
-            return sq
+                nc.scalar.activation(out=sq[(m, u)][:, cols], in_=acc[:], func=ACT.Square, bias=bias0[:])
 
-        def amplitude(sq_e, sq_o, idx, parts):
-            ss = sq_o
-            h = ring.tile([P, S], F32, name="h", tag="h", bufs=CFG["hb"])
-            if ADD_ON[idx] == "p":
-                for half in range(2):
-                    acc = psum.tile([P, BANK], F32, name="acc", tag=TAG2, bufs=BUF2)
-                    for j0 in range(0, BANK, P):
-                        jt = (half * BANK + j0) // P
-                        nc.tensor.matmul(acc[:, j0 : j0 + P], sq_e[:, jt, :], ident[:], start=True, stop=False, is_transpose=True)
-                        nc.tensor.matmul(acc[:, j0 : j0 + P], sq_o[:, jt, :], ident[:], start=False, stop=True, is_transpose=True)
-                    nc.scalar.activation(out=h[:, half * BANK : (half + 1) * BANK], in_=acc[:], func=ACT.Sqrt)
-                return h
+        def square_cols(m, u, count=1):
+            b, t = divmod(u, PACK)
+            width = count * P
+            per = BANK // width
+            tiles = [sca_tile([P, S // P // count, width], F32, "sq%s%d" % (m, u)) for c in range(count)]
+            for j0 in range(0, S // P, per):
+                acc = bank([P, per, width])
+                for jj in range(per):
+                    js = slice((j0 + jj) * P, (j0 + jj + 1) * P)
+                    for a in range(2):
+                        key = "%s%d%d" % (m, a, b)
+                        nc.tensor.matmul_mx(
+                            out=acc[:, jj, :],
+                            lhsT=v_t[a][:, js].bitcast(FP8X4),
+                            lhsT_scale=vs_t[4 * a : P, js],
+                            rhs=codes[key][:, t * P : t * P + width].bitcast(FP8X4),
+                            rhs_scale=scales[key][:, t * P : t * P + width],
+                            start=(a == 0),
+                            stop=(a == 1),
+                        )
+                c, jl = divmod(j0, S // P // count)
+                nc.scalar.activation(out=tiles[c][:, jl : jl + per, :], in_=acc[:], func=ACT.Square, bias=bias0[:])
+            for c in range(count):
+                sq[(m, u + c)] = [tiles[j // (S // P // count)][:, j % (S // P // count), c * P : (c + 1) * P] for j in range(S // P)]
+
+        def root_cols(u):
+            hs[u] = sca_tile([P, S], F32, "h%d" % u)
+            for half in range(2):
+                acc = bank([P, BANK])
+                for j0 in range(0, BANK, P):
+                    jt = (half * BANK + j0) // P
+                    nc.tensor.matmul(acc[:, j0 : j0 + P], sq[("e", u)][jt], ident[:], start=True, stop=False, is_transpose=True)
+                    nc.tensor.matmul(acc[:, j0 : j0 + P], sq[("o", u)][jt], ident[:], start=False, stop=True, is_transpose=True)
+                nc.scalar.activation(out=hs[u][:, half * BANK : (half + 1) * BANK], in_=acc[:], func=ACT.Sqrt)
+
+        def root_rows(u, parts=2, eng="v"):
+            ss = vec_tile([P, S], F32, "ss%d" % u)
+            hs[u] = sca_tile([P, S], F32, "h%d" % u)
             w = S // parts
             for c in range(parts):
                 cols = slice(c * w, (c + 1) * w)
-                if ADD_ON[idx][c % len(ADD_ON[idx])] == "v":
-                    nc.vector.tensor_tensor(out=ss[:, cols], in0=sq_e[:, cols], in1=sq_o[:, cols], op=ALU.add)
-                else:
-                    for c0 in range(c * w, (c + 1) * w, 256):
-                        piece = slice(c0, c0 + 256)
-                        nc.gpsimd.tensor_tensor(out=ss[:, piece], in0=sq_e[:, piece], in1=sq_o[:, piece], op=ALU.add)
-                nc.scalar.activation(out=h[:, cols], in_=ss[:, cols], func=ACT.Sqrt)
-            return h
+                adder = nc.vector if eng == "v" else nc.gpsimd
+                adder.tensor_tensor(out=ss[:, cols], in0=sq[("e", u)][:, cols], in1=sq[("o", u)][:, cols], op=ALU.add)
+                nc.scalar.activation(out=hs[u][:, cols], in_=ss[:, cols], func=ACT.Sqrt)
 
-        def pick(h, dst, t, lst, lo, hi):
-            nc.vector.tensor_copy(out=dst[:, t, lo:hi], in_=h[:].indirect(lst[:, lo // 16 : hi // 16]))
+        later = {}
 
-        def difference(ha, hb, b, lo, hi):
-            z = ring.tile([P, (hi - lo) * PACK], BF16, name="z", tag="z%d" % b, bufs=2, align_bytes=64)
-            eng = nc.vector if SUB_ON[b] == "v" else nc.gpsimd
-            eng.tensor_tensor(
-                out=z[:].rearrange("p (c i t) -> p c t i", i=4, t=PACK),
-                in0=ha[:, :, lo:hi].rearrange("p t (c i) -> p c t i", i=4),
-                in1=hb[:, :, lo:hi].rearrange("p t (c i) -> p c t i", i=4),
-                op=ALU.subtract,
+        def pick_second(u, lo=0, hi=NPAIR):
+            later[(u, lo)] = vec_tile([P, hi - lo], F32, "hb%d" % u)
+            nc.vector.tensor_copy(out=later[(u, lo)][:], in_=hs[u][:].indirect(pos2_t[:, lo // 16 : hi // 16]))
+
+        def pick_first(u, lo=0, hi=NPAIR):
+            b, t = divmod(u, PACK)
+            nc.vector.tensor_tensor(
+                out=diff[b][:, t, lo:hi], in0=hs[u][:].indirect(pos1_t[:, lo // 16 : hi // 16]), in1=later[(u, lo)][:], op=ALU.subtract
             )
-            return z
 
-        def diff_rows(ha, hb, t, lo, hi):
-            nc.vector.tensor_tensor(out=ha[:, t, lo:hi], in0=ha[:, t, lo:hi], in1=hb[:, t, lo:hi], op=ALU.subtract)
+        zs = {}
 
-        def weave(ha, b, lo, hi, eng):
-            z = ring.tile([P, (hi - lo) * PACK], BF16, name="z", tag="z%d" % b, bufs=2, align_bytes=64)
+        def weave(b, lo, hi, eng):
+            make = sca_tile if eng == "s" else vec_tile
+            z = make([P, (hi - lo) * PACK], BF16, "z%d" % b)
+            zs[(b, lo)] = z
             dst = z[:].rearrange("p (c i t) -> p c t i", i=4, t=PACK)
-            src = ha[:, :, lo:hi].rearrange("p t (c i) -> p c t i", i=4)
+            src = diff[b][:, :, lo:hi].rearrange("p t (c i) -> p c t i", i=4)
             if eng == "s":
                 nc.scalar.copy(out=dst, in_=src)
-            else:
+            elif eng == "v":
                 nc.vector.tensor_copy(out=dst, in_=src)
-            return z
+            else:
+                nc.gpsimd.tensor_scalar(out=dst, in0=src, scalar1=1.0, scalar2=0.0, op0=ALU.mult, op1=ALU.add)
 
-        def quant_z(z, b, lo, hi):
-            nc.vector.quantize_mx(
-                out=z_codes[b][:, lo:hi].bitcast(FP8X4), scales=z_scales[b][:, lo:hi], in_=z[:]
-            )
+        def quant_z(b, lo, hi):
+            nc.vector.quantize_mx(out=z_codes[b][:, lo:hi].bitcast(FP8X4), scales=z_scales[b][:, lo:hi], in_=zs[(b, lo)][:])
 
         out_v = out.rearrange("(g p) i -> p g i", p=P)
 
@@ -256,90 +228,133 @@ def tile_list_quadrature_motion_readout_kernel(
                 stop=(a == 1),
             )
 
-        def readout_split(lo, accs):
-            res = ring.tile([P, N // P, P], F32, name="res", tag="res", bufs=4)
+        def readout(lo):
+            res = ring.tile([P, N // P, P], F32, name="res", tag="res", bufs=PIECES)
+            acc = bank([P, N // P, P])
+            for g in range(N // P):
+                for a in range(2):
+                    w2_pass(acc[:, g, :], g, a, lo)
+            nc.scalar.copy(out=res[:], in_=acc[:])
+            nc.sync.dma_start(out=out_v[:, :, lo : lo + P], in_=res[:])
+
+        def readout_last(lo, accs):
+            res = ring.tile([P, N // P, P], F32, name="res", tag="res", bufs=PIECES)
             for g in range(N // P):
                 w2_pass(accs[g][:], g, 1, lo)
                 if g % 2 == 0:
                     nc.scalar.copy(out=res[:, g, :], in_=accs[g][:])
                 else:
                     nc.vector.tensor_copy(out=res[:, g, :], in_=accs[g][:])
-                if CFG["st2"] and g % 2 == 1:
-                    nc.sync.dma_start(out=out_v[:, g - 1 : g + 1, lo : lo + P], in_=res[:, g - 1 : g + 1, :])
-            if not CFG["st2"]:
-                nc.sync.dma_start(out=out_v[:, :, lo : lo + P], in_=res[:])
+            nc.sync.dma_start(out=out_v[:, :, lo : lo + P], in_=res[:])
 
-        def readout(lo, hi, eng):
-            res = ring.tile([P, N // P, hi - lo], F32, name="res", tag="res", bufs=4)
-            for c0 in range(lo, hi, P):
-                acc = psum.tile([P, N // P, P], F32, name="acc", tag=TAG2, bufs=BUF2)
-                for g in range(N // P):
-                    for a in range(2):
-                        nc.tensor.matmul_mx(
-                            out=acc[:, g, :],
-                            lhsT=w2_t[:, a, 2 * g * P : 2 * (g + 1) * P].bitcast(FP4X4),
-                            lhsT_scale=w2s_t[:, a, g * P : (g + 1) * P],
-                            rhs=z_codes[a][:, c0 : c0 + P].bitcast(FP8X4),
-                            rhs_scale=z_scales[a][:, c0 : c0 + P],
-                            start=(a == 0),
-                            stop=(a == 1),
-                        )
-                if eng == "s":
-                    nc.scalar.copy(out=res[:, :, c0 - lo : c0 - lo + P], in_=acc[:])
-                else:
-                    nc.vector.tensor_copy(out=res[:, :, c0 - lo : c0 - lo + P], in_=acc[:])
-            nc.sync.dma_start(out=out_v[:, :, lo:hi], in_=res[:])
+        def load_w2():
+            nc.sync.dma_start(out=w2_t[:].bitcast(I32), in_=w2_words.rearrange("a p c -> p a c").bitcast(I32))
+            for q in range(4):
+                nc.sync.dma_start(
+                    out=w2s_t[32 * q : 32 * q + 4, :, :].bitcast(I32),
+                    in_=w2_scales[:, 4 * q : 4 * q + 4, :].rearrange("a r n -> r a n").bitcast(I32),
+                )
 
-        picks = {}
-        hs = {}
-        sqs = {}
-        for tok in CFG["order"]:
-            kind = tok[0]
-            if kind == "c":
-                cast((tok[1], int(tok[2]), int(tok[3])))
-            elif kind == "q":
-                quant_w((tok[1], int(tok[2]), int(tok[3])), CFG["qp"].get(tok[1:], 1))
-            elif kind == "s":
-                nc.vector.tensor_copy(out=vs_t[:], in_=tabs_t[:].bitcast(U8).indirect(offs_t[:]))
-            elif kind == "t":
-                gather_tab(int(tok[1]), int(tok[2]))
-            elif kind in "EO":
-                u = int(tok[1])
-                sqs[tok] = square("e" if kind == "E" else "o", u // PACK, u % PACK)
-            elif kind == "A":
-                u = int(tok[1])
-                hs[u] = amplitude(sqs["E%d" % u], sqs["O%d" % u], u, CFG["ap"][u])
-            elif kind in "GH":
-                u = int(tok[1])
-                side = 0 if kind == "G" else 1
-                key = (u // PACK, side)
-                if key not in picks:
-                    picks[key] = ring.tile([P, PACK, NPAIR], F32, name="pick%d%d" % key, tag="pick", bufs=4, align_bytes=64)
-                pick(hs[u], picks[key], u % PACK, (pos1_t, pos2_t)[side], 0, NPAIR)
-            else:
-                c = int(tok[1])
-                lo, hi = c * NPAIR // 2, (c + 1) * NPAIR // 2
-                if kind == "Z":
-                    zs0[c] = difference(picks[(0, 0)], picks[(0, 1)], 0, lo, hi)
-                else:
-                    quant_z(zs0[c], 0, lo, hi)
-        picks = [[picks[(b, u)] for u in range(2)] for b in range(2)]
-        h = hs[2 * PACK - 1]
-        w = NPAIR // TAIL
-        for c in range(TAIL):
+        def gather_scales():
+            nc.vector.tensor_copy(out=vs_t[:], in_=tabs_t[:].bitcast(U8).indirect(offs_t[:]))
+
+        make_identity(nc, ident[:])
+        nc.vector.memset(tabs_t[:], 0)
+        nc.vector.memset(zero[:], 0.0)
+        nc.vector.memset(w2s_t[:].rearrange("p a n -> p (a n)").bitcast(I32), 0)
+        nc.scalar.activation(out=bias0[:], in_=zero[:], func=ACT.Sqrt)
+
+        load_tab(0)
+        load_scales((0, 1))
+        nc.sync.dma_start(out=offs_t[:], in_=offs)
+        load_w("e00")
+        load_scales((2, 3))
+        load_w("e10")
+        load_tab(1)
+        load_w("o00")
+        load_w("o10", 2)
+        nc.sync.dma_start(out=pos2_t[:], in_=pos2)
+        nc.sync.dma_start(out=pos1_t[:], in_=pos1)
+        for key in ("e01", "e11", "o01", "o11"):
+            load_w(key)
+        load_w2()
+
+        gather_tab(0, 0)
+        gather_tab(0, 1)
+        cast("e00", "s")
+        gather_scales()
+        quant_w("e00")
+        cast("e10", "s")
+        quant_w("e10")
+        gather_tab(1, 0)
+        gather_tab(1, 1)
+        square_rows("e", 0)
+        square_cols("e", 1)
+        cast("o00", "v")
+        square_cols("e", 2, 2)
+        cast("o10", "vv")
+        quant_w("o00", 0, 1)
+        quant_w("o10", 0, 1)
+        square_rows("o", 0)
+        quant_w("o00", 1, 2)
+        quant_w("o10", 1, 2)
+        square_cols("o", 1)
+        quant_w("o00", 2, 4)
+        quant_w("o10", 2, 4)
+        cast("e01", "v")
+        root_rows(0)
+        quant_w("e01")
+        square_cols("o", 2, 2)
+        cast("e11", "v")
+        root_cols(1)
+        pick_second(0)
+        quant_w("e11")
+        cast("o01", "v")
+        pick_first(0)
+        root_cols(2)
+        root_cols(3)
+        quant_w("o01")
+        cast("o11", "v")
+        pick_second(1)
+        square_cols("e", 4, 2)
+        quant_w("o11")
+        pick_second(2)
+        pick_first(1)
+        square_cols("e", 6, 2)
+        square_cols("o", 4, 2)
+        pick_second(3)
+        pick_first(2)
+        root_cols(4)
+        pick_first(3)
+        pick_second(4)
+        root_cols(5)
+        square_cols("o", 6, 2)
+        w = NPAIR // PIECES
+        pick_second(5)
+        pick_first(4)
+        root_cols(6)
+        root_cols(7)
+        pick_first(5)
+        weave(0, 0, 2 * w, "v")
+        weave(0, 2 * w, 4 * w, "s")
+        pick_second(6, 0, w)
+        quant_z(0, 0, 2 * w)
+        for c in range(PIECES):
             lo, hi = c * w, (c + 1) * w
-            pick(h, picks[1][0], PACK - 1, pos1_t, lo, hi)
-            pick(h, picks[1][1], PACK - 1, pos2_t, lo, hi)
-            if CFG["weave"]:
-                diff_rows(picks[1][0], picks[1][1], PACK - 1, lo, hi)
-                quant_z(weave(picks[1][0], 1, lo, hi, CFG["weave"][c]), 1, lo, hi)
-            else:
-                quant_z(difference(picks[1][0], picks[1][1], 1, lo, hi), 1, lo, hi)
-            if c == TAIL - 2 and CFG["pre"]:
-                accs = [psum.tile([P, P], F32, name="acc", tag="acc", bufs=CFG["mmb"]) for g in range(N // P)]
-                for g in range(N // P):
-                    w2_pass(accs[g][:], g, 0, NPAIR - P)
-            if c == TAIL - 1 and CFG["pre"]:
-                readout_split(lo, accs)
-            else:
-                readout(lo, hi, CFG["rescopy"][c])
+            pick_second(7, lo, hi)
+            pick_first(6, lo, hi)
+            if c + 1 < PIECES:
+                pick_second(6, hi, hi + w)
+            pick_first(7, lo, hi)
+            if c == 1:
+                quant_z(0, 2 * w, 4 * w)
+            if c > 0:
+                quant_z(1, lo - w, lo)
+            weave(1, lo, hi, "s" if c + 1 < PIECES else "v")
+            if c > 0:
+                readout(lo - w)
+        accs = [bank([P, P]) for g in range(N // P)]
+        for g in range(N // P):
+            w2_pass(accs[g][:], g, 0, NPAIR - P)
+        quant_z(1, NPAIR - w, NPAIR)
+        readout_last(NPAIR - w, accs)

@@ -22,7 +22,7 @@ PACK = 4
 KP = P * PACK
 BANK = 512
 RAW_BUFS = 4
-VEC_BUFS = 6
+VEC_BUFS = 15
 SCA_BUFS = 12
 PIECES = 4
 
@@ -49,14 +49,6 @@ def tile_list_quadrature_motion_readout_kernel(
         bias0 = keep.tile([P, 1], F32, name="bias0")
         w_in = {"e": we, "o": wo}
         raw, codes, scales, grouped = {}, {}, {}, {}
-        for m in "eo":
-            for a in range(2):
-                for b in range(2):
-                    key = "%s%d%d" % (m, a, b)
-                    codes[key] = keep.tile([P, KP], U32, name="wc" + key, align_bytes=64)
-                    scales[key] = keep.tile([P, KP], U8, name="ws" + key, align_bytes=64)
-        z_codes = [keep.tile([P, NPAIR], U32, name="zc%d" % b, align_bytes=64) for b in range(2)]
-        z_scales = [keep.tile([P, NPAIR], U8, name="zs%d" % b, align_bytes=64) for b in range(2)]
         diff = [keep.tile([P, PACK, NPAIR], F32, name="diff%d" % b, align_bytes=64) for b in range(2)]
         ident = keep.tile([P, P], F32, name="ident")
 
@@ -87,13 +79,16 @@ def tile_list_quadrature_motion_readout_kernel(
                 for a in range(2):
                     nc.sync.dma_start(out=tabs_t[4 * a + r : P : 32, :], in_=tab_scales[a, r:16:4, :].bitcast(I32))
 
-        def cast(key, engines):
+        def cast(key, engines, only=None):
             make = sca_tile if engines[0] == "s" else vec_tile
-            g = make([P, PACK, P, PACK], BF16, "g" + key)
-            grouped[key] = g
+            if key not in grouped:
+                grouped[key] = make([P, PACK, P, PACK], BF16, "g" + key)
+            g = grouped[key]
             rows = P // len(engines)
             per_load = P // len(raw[key])
             for h, eng in enumerate(engines):
+                if only is not None and h != only:
+                    continue
                 m0 = h * rows
                 r = raw[key][m0 // per_load]
                 c0 = (m0 % per_load) * PACK
@@ -108,11 +103,12 @@ def tile_list_quadrature_motion_readout_kernel(
 
         def quant_w(key, t0=0, t1=PACK):
             flat = grouped[key][:].rearrange("p t m j -> p (t m j)")
-            nc.vector.quantize_mx(
-                out=codes[key][:, t0 * P : t1 * P].bitcast(FP8X4),
-                scales=scales[key][:, t0 * P : t1 * P],
-                in_=flat[:, t0 * KP : t1 * KP],
-            )
+            c = vec_tile([P, (t1 - t0) * P], U32, "wc" + key)
+            s = keep.tile([P, (t1 - t0) * P], U8, name="ws%s%d" % (key, t0), align_bytes=64)
+            nc.vector.quantize_mx(out=c[:].bitcast(FP8X4), scales=s[:], in_=flat[:, t0 * KP : t1 * KP])
+            for t in range(t0, t1):
+                codes[(key, t)] = c[:, (t - t0) * P :]
+                scales[(key, t)] = s[:, (t - t0) * P :]
 
         def gather_tab(a, half):
             cols = slice(half * BANK, (half + 1) * BANK)
@@ -121,59 +117,96 @@ def tile_list_quadrature_motion_readout_kernel(
 
         sq, hs = {}, {}
 
-        def square_rows(m, u):
-            b, t = divmod(u, PACK)
-            sq[(m, u)] = sca_tile([P, S], F32, "sq%s%d" % (m, u))
-            for half in range(2):
-                cols = slice(half * BANK, (half + 1) * BANK)
-                acc = bank([P, BANK])
-                for a in range(2):
-                    key = "%s%d%d" % (m, a, b)
-                    nc.tensor.matmul_mx(
-                        out=acc[:],
-                        lhsT=codes[key][:, t * P : (t + 1) * P].bitcast(FP8X4),
-                        lhsT_scale=scales[key][:, t * P : (t + 1) * P],
-                        rhs=v_t[a][:, cols].bitcast(FP8X4),
-                        rhs_scale=vs_t[4 * a : P, cols],
-                        start=(a == 0),
-                        stop=(a == 1),
-                    )
-                nc.scalar.activation(out=sq[(m, u)][:, cols], in_=acc[:], func=ACT.Square, bias=bias0[:])
+        opened = {}
 
-        def square_cols(m, u, count=1):
+        def rows_pass(acc, m, u, half, a):
             b, t = divmod(u, PACK)
-            width = count * P
-            per = BANK // width
-            tiles = [sca_tile([P, S // P // count, width], F32, "sq%s%d" % (m, u)) for c in range(count)]
-            for j0 in range(0, S // P, per):
-                acc = bank([P, per, width])
+            cols = slice(half * BANK, (half + 1) * BANK)
+            key = "%s%d%d" % (m, a, b)
+            nc.tensor.matmul_mx(
+                out=acc[:],
+                lhsT=codes[(key, t)][:, :P].bitcast(FP8X4),
+                lhsT_scale=scales[(key, t)][:, :P],
+                rhs=v_t[a][:, cols].bitcast(FP8X4),
+                rhs_scale=vs_t[4 * a : P, cols],
+                start=(a == 0),
+                stop=(a == 1),
+            )
+
+        def open_rows(m, u):
+            for half in range(2):
+                opened[(m, u, half)] = bank([P, BANK])
+                rows_pass(opened[(m, u, half)], m, u, half, 0)
+
+        def square_rows(m, u, halves=(0, 1), **bias):
+            if 0 in halves:
+                sq[(m, u)] = sca_tile([P, S], F32, "sq%s%d" % (m, u))
+            for half in halves:
+                if (m, u, half) in opened:
+                    acc = opened[(m, u, half)]
+                else:
+                    acc = bank([P, BANK])
+                    rows_pass(acc, m, u, half, 0)
+                rows_pass(acc, m, u, half, 1)
+                nc.scalar.activation(out=sq[(m, u)][:, half * BANK : (half + 1) * BANK], in_=acc[:], func=ACT.Square, **bias)
+
+        cols_tiles = {}
+
+        def cols_pass(acc, m, u, count, j, a):
+            b, t = divmod(u, PACK)
+            js = slice(j * P, (j + 1) * P)
+            key = "%s%d%d" % (m, a, b)
+            nc.tensor.matmul_mx(
+                out=acc,
+                lhsT=v_t[a][:, js].bitcast(FP8X4),
+                lhsT_scale=vs_t[4 * a : P, js],
+                rhs=codes[(key, t)][:, : count * P].bitcast(FP8X4),
+                rhs_scale=scales[(key, t)][:, : count * P],
+                start=(a == 0),
+                stop=(a == 1),
+            )
+
+        def cols_square(acc, m, u, count, j0, **bias):
+            per = PACK // count
+            c, jl = divmod(j0, 2 * per)
+            if jl == 0:
+                cols_tiles[(m, u, c)] = sca_tile([P, 2 * per, count * P], F32, "sq%s%d" % (m, u))
+            tile = cols_tiles[(m, u, c)]
+            nc.scalar.activation(out=tile[:, jl : jl + per, :], in_=acc[:], func=ACT.Square, **bias)
+            for d in range(count):
                 for jj in range(per):
-                    js = slice((j0 + jj) * P, (j0 + jj + 1) * P)
-                    for a in range(2):
-                        key = "%s%d%d" % (m, a, b)
-                        nc.tensor.matmul_mx(
-                            out=acc[:, jj, :],
-                            lhsT=v_t[a][:, js].bitcast(FP8X4),
-                            lhsT_scale=vs_t[4 * a : P, js],
-                            rhs=codes[key][:, t * P : t * P + width].bitcast(FP8X4),
-                            rhs_scale=scales[key][:, t * P : t * P + width],
-                            start=(a == 0),
-                            stop=(a == 1),
-                        )
-                c, jl = divmod(j0, S // P // count)
-                nc.scalar.activation(out=tiles[c][:, jl : jl + per, :], in_=acc[:], func=ACT.Square, bias=bias0[:])
-            for c in range(count):
-                sq[(m, u + c)] = [tiles[j // (S // P // count)][:, j % (S // P // count), c * P : (c + 1) * P] for j in range(S // P)]
+                    sq[(m, u + d, j0 + jj)] = tile[:, jl + jj, d * P : (d + 1) * P]
+
+        def open_cols(m, u, count):
+            per = PACK // count
+            for j0 in range(0, S // P, per):
+                opened[(m, u, j0)] = bank([P, per, count * P])
+                cols_pass(opened[(m, u, j0)][:, 0, :], m, u, count, j0, 0)
+
+        def square_cols(m, u, count=1, part=0, parts=1, **bias):
+            per = PACK // count
+            span = S // P // parts
+            for j0 in range(part * span, (part + 1) * span, per):
+                ahead = (m, u, j0) in opened
+                acc = opened[(m, u, j0)] if ahead else bank([P, per, count * P])
+                for jj in range(per):
+                    for a in range(1 if ahead and jj == 0 else 0, 2):
+                        cols_pass(acc[:, jj, :], m, u, count, j0 + jj, a)
+                cols_square(acc, m, u, count, j0, **bias)
+
+        def root_half(u, half):
+            if half == 0:
+                hs[u] = sca_tile([P, S], F32, "h%d" % u)
+            acc = bank([P, BANK])
+            for j0 in range(0, BANK, P):
+                jt = (half * BANK + j0) // P
+                nc.tensor.matmul(acc[:, j0 : j0 + P], sq[("e", u, jt)], ident[:], start=True, stop=False, is_transpose=True)
+                nc.tensor.matmul(acc[:, j0 : j0 + P], sq[("o", u, jt)], ident[:], start=False, stop=True, is_transpose=True)
+            nc.scalar.activation(out=hs[u][:, half * BANK : (half + 1) * BANK], in_=acc[:], func=ACT.Sqrt)
 
         def root_cols(u):
-            hs[u] = sca_tile([P, S], F32, "h%d" % u)
-            for half in range(2):
-                acc = bank([P, BANK])
-                for j0 in range(0, BANK, P):
-                    jt = (half * BANK + j0) // P
-                    nc.tensor.matmul(acc[:, j0 : j0 + P], sq[("e", u)][jt], ident[:], start=True, stop=False, is_transpose=True)
-                    nc.tensor.matmul(acc[:, j0 : j0 + P], sq[("o", u)][jt], ident[:], start=False, stop=True, is_transpose=True)
-                nc.scalar.activation(out=hs[u][:, half * BANK : (half + 1) * BANK], in_=acc[:], func=ACT.Sqrt)
+            root_half(u, 0)
+            root_half(u, 1)
 
         def root_rows(u, parts=2, eng="v"):
             ss = vec_tile([P, S], F32, "ss%d" % u)
@@ -212,8 +245,15 @@ def tile_list_quadrature_motion_readout_kernel(
             else:
                 nc.gpsimd.tensor_scalar(out=dst, in0=src, scalar1=1.0, scalar2=0.0, op0=ALU.mult, op1=ALU.add)
 
+        z_codes, z_scales = {}, {}
+
         def quant_z(b, lo, hi):
-            nc.vector.quantize_mx(out=z_codes[b][:, lo:hi].bitcast(FP8X4), scales=z_scales[b][:, lo:hi], in_=zs[(b, lo)][:])
+            c = vec_tile([P, hi - lo], U32, "zc%d" % b)
+            s = keep.tile([P, hi - lo], U8, name="zs%d_%d" % (b, lo), align_bytes=64)
+            nc.vector.quantize_mx(out=c[:].bitcast(FP8X4), scales=s[:], in_=zs[(b, lo)][:])
+            for c0 in range(lo, hi, P):
+                z_codes[(b, c0)] = c[:, c0 - lo : c0 - lo + P]
+                z_scales[(b, c0)] = s[:, c0 - lo : c0 - lo + P]
 
         out_v = out.rearrange("(g p) i -> p g i", p=P)
 
@@ -222,14 +262,14 @@ def tile_list_quadrature_motion_readout_kernel(
                 out=acc,
                 lhsT=w2_t[:, a, 2 * g * P : 2 * (g + 1) * P].bitcast(FP4X4),
                 lhsT_scale=w2s_t[:, a, g * P : (g + 1) * P],
-                rhs=z_codes[a][:, c0 : c0 + P].bitcast(FP8X4),
-                rhs_scale=z_scales[a][:, c0 : c0 + P],
+                rhs=z_codes[(a, c0)].bitcast(FP8X4),
+                rhs_scale=z_scales[(a, c0)],
                 start=(a == 0),
                 stop=(a == 1),
             )
 
         def readout(lo):
-            res = ring.tile([P, N // P, P], F32, name="res", tag="res", bufs=PIECES)
+            res = sca_tile([P, N // P, P], F32, "res")
             acc = bank([P, N // P, P])
             for g in range(N // P):
                 for a in range(2):
@@ -238,7 +278,7 @@ def tile_list_quadrature_motion_readout_kernel(
             nc.sync.dma_start(out=out_v[:, :, lo : lo + P], in_=res[:])
 
         def readout_last(lo, accs):
-            res = ring.tile([P, N // P, P], F32, name="res", tag="res", bufs=PIECES)
+            res = sca_tile([P, N // P, P], F32, "res")
             for g in range(N // P):
                 w2_pass(accs[g][:], g, 1, lo)
                 if g % 2 == 0:
@@ -267,9 +307,9 @@ def tile_list_quadrature_motion_readout_kernel(
         load_tab(0)
         load_scales((0, 1))
         nc.sync.dma_start(out=offs_t[:], in_=offs)
-        load_w("e00")
-        load_scales((2, 3))
         load_w("e10")
+        load_scales((2, 3))
+        load_w("e00")
         load_tab(1)
         load_w("o00")
         load_w("o10", 2)
@@ -281,25 +321,33 @@ def tile_list_quadrature_motion_readout_kernel(
 
         gather_tab(0, 0)
         gather_tab(0, 1)
-        cast("e00", "s")
-        gather_scales()
-        quant_w("e00")
         cast("e10", "s")
+        gather_scales()
         quant_w("e10")
+        cast("e00", "s")
+        quant_w("e00")
+        open_rows("e", 0)
+        open_cols("e", 1, 1)
+        open_cols("e", 2, 2)
         gather_tab(1, 0)
         gather_tab(1, 1)
-        square_rows("e", 0)
-        square_cols("e", 1)
+        square_rows("e", 0, (0,), bias=bias0[:])
+        square_cols("e", 1, 1, 0, 2)
+        square_cols("e", 2, 2, 0, 2)
+        square_rows("e", 0, (1,))
+        square_cols("e", 1, 1, 1, 2)
         cast("o00", "v")
-        square_cols("e", 2, 2)
-        cast("o10", "vv")
-        quant_w("o00", 0, 1)
+        square_cols("e", 2, 2, 1, 2)
+        cast("o10", "vv", 0)
+        quant_w("o00", 0, 2)
+        open_rows("o", 0)
+        open_cols("o", 1, 1)
+        cast("o10", "vv", 1)
+        quant_w("o00", 2, 4)
         quant_w("o10", 0, 1)
         square_rows("o", 0)
-        quant_w("o00", 1, 2)
         quant_w("o10", 1, 2)
         square_cols("o", 1)
-        quant_w("o00", 2, 4)
         quant_w("o10", 2, 4)
         cast("e01", "v")
         root_rows(0)

@@ -25,6 +25,7 @@ RAW_BUFS = 4
 VEC_BUFS = 15
 SCA_BUFS = 12
 PIECES = 4
+PAIR = 2 * P
 
 
 def tile_list_quadrature_motion_readout_kernel(
@@ -194,6 +195,37 @@ def tile_list_quadrature_motion_readout_kernel(
                         cols_pass(acc[:, jj, :], m, u, count, j0 + jj, a)
                 cols_square(acc, m, u, count, j0, **bias)
 
+        def cast_pairs(key, eng="v"):
+            make = sca_tile if eng == "s" else vec_tile
+            grouped[key] = make([P, 2, P, 2, PACK], BF16, "g" + key)
+            dst = grouped[key][:].rearrange("p u m t j -> p m u j t")
+            src = raw[key][0][:].rearrange("p j (m u t) -> p m u j t", u=2, t=2)
+            if eng == "v":
+                nc.vector.tensor_copy(out=dst, in_=src)
+            else:
+                nc.scalar.copy(out=dst, in_=src)
+
+        def quant_pairs(key):
+            c = vec_tile([P, KP], U32, "wc" + key)
+            s = keep.tile([P, KP], U8, name="ws" + key, align_bytes=64)
+            nc.vector.quantize_mx(out=c[:].bitcast(FP8X4), scales=s[:], in_=grouped[key][:].rearrange("p u m t j -> p (u m t j)"))
+            for t in (0, 2):
+                codes[(key, t)] = c[:, t * P :]
+                scales[(key, t)] = s[:, t * P :]
+
+        def square_pair(m, u):
+            for half in range(2):
+                tile = sca_tile([P, 4, 2, P], F32, "sq%s%d" % (m, u))
+                for jl in (0, 2):
+                    acc = bank([P, 2, PAIR])
+                    for jj in range(2):
+                        for a in range(2):
+                            cols_pass(acc[:, jj, :], m, u, 2, 4 * half + jl + jj, a)
+                    nc.scalar.activation(out=tile[:, jl : jl + 2, :, :], in_=acc[:].rearrange("p j (m t) -> p j t m", t=2), func=ACT.Square)
+                for jl in range(4):
+                    for t in range(2):
+                        sq[(m, u + t, 4 * half + jl)] = tile[:, jl, t, :]
+
         def root_half(u, half):
             if half == 0:
                 hs[u] = sca_tile([P, S], F32, "h%d" % u)
@@ -349,34 +381,34 @@ def tile_list_quadrature_motion_readout_kernel(
         quant_w("o10", 1, 2)
         square_cols("o", 1)
         quant_w("o10", 2, 4)
-        cast("e01", "v")
+        cast_pairs("e01", "v")
         root_rows(0)
-        quant_w("e01")
+        quant_pairs("e01")
         square_cols("o", 2, 2)
-        cast("e11", "v")
+        cast_pairs("e11", "v")
         root_cols(1)
         pick_second(0)
-        quant_w("e11")
-        cast("o01", "v")
+        quant_pairs("e11")
+        cast_pairs("o01", "v")
         pick_first(0)
         root_cols(2)
         root_cols(3)
-        quant_w("o01")
-        cast("o11", "v")
+        quant_pairs("o01")
+        cast_pairs("o11", "v")
         pick_second(1)
-        square_cols("e", 4, 2)
-        quant_w("o11")
+        square_pair("e", 4)
+        quant_pairs("o11")
         pick_second(2)
         pick_first(1)
-        square_cols("e", 6, 2)
-        square_cols("o", 4, 2)
+        square_pair("e", 6)
+        square_pair("o", 4)
         pick_second(3)
         pick_first(2)
         root_cols(4)
         pick_first(3)
         pick_second(4)
         root_cols(5)
-        square_cols("o", 6, 2)
+        square_pair("o", 6)
         w = NPAIR // PIECES
         pick_second(5)
         pick_first(4)
@@ -396,13 +428,16 @@ def tile_list_quadrature_motion_readout_kernel(
             pick_first(7, lo, hi)
             if c == 1:
                 quant_z(0, 2 * w, 4 * w)
+                accs = [bank([P, P]) for g in range(N // P)]
+                for g in range(N // P):
+                    w2_pass(accs[g][:], g, 0, NPAIR - P)
+            if c + 1 < PIECES:
+                weave(1, lo, hi, "s")
             if c > 0:
                 quant_z(1, lo - w, lo)
-            weave(1, lo, hi, "s" if c + 1 < PIECES else "v")
-            if c > 0:
-                readout(lo - w)
-        accs = [bank([P, P]) for g in range(N // P)]
-        for g in range(N // P):
-            w2_pass(accs[g][:], g, 0, NPAIR - P)
+            if c > 1:
+                readout(lo - 2 * w)
+        weave(1, NPAIR - w, NPAIR, "v")
+        readout(NPAIR - 2 * w)
         quant_z(1, NPAIR - w, NPAIR)
         readout_last(NPAIR - w, accs)

@@ -317,7 +317,7 @@ def tile_list_quadrature_motion_readout_kernel(
                     nc.scalar.copy(out=res[:, g, :], in_=accs[g][:])
                 else:
                     nc.vector.tensor_copy(out=res[:, g, :], in_=accs[g][:])
-            nc.sync.dma_start(out=out_v[:, :, lo : lo + P], in_=res[:])
+                    nc.sync.dma_start(out=out_v[:, g - 1 : g + 1, lo : lo + P], in_=res[:, g - 1 : g + 1, :])
 
         def load_w2():
             nc.sync.dma_start(out=w2_t[:].bitcast(I32), in_=w2_words.rearrange("a p c -> p a c").bitcast(I32))
@@ -415,7 +415,7 @@ def tile_list_quadrature_motion_readout_kernel(
         root_cols(6)
         root_cols(7)
         pick_first(5)
-        weave(0, 0, 2 * w, "v")
+        weave(0, 0, 2 * w, "s")
         weave(0, 2 * w, 4 * w, "s")
         pick_second(6, 0, w)
         quant_z(0, 0, 2 * w)

@@ -21,11 +21,13 @@ P = 128
 PACK = 4
 KP = P * PACK
 BANK = 512
-RAW_BUFS = 4
+RAW_BUFS = 3
+RAWG_BUFS = 5
 VEC_BUFS = 15
 SCA_BUFS = 12
 PIECES = 4
 PAIR = 2 * P
+HALF = P // 2
 
 
 def tile_list_quadrature_motion_readout_kernel(
@@ -51,6 +53,7 @@ def tile_list_quadrature_motion_readout_kernel(
         w_in = {"e": we, "o": wo}
         raw, codes, scales, grouped = {}, {}, {}, {}
         diff = [keep.tile([P, PACK, NPAIR], F32, name="diff%d" % b, align_bytes=64) for b in range(2)]
+        spare = keep.tile([P, 2, NPAIR], F32, name="spare", align_bytes=64)
         ident = keep.tile([P, P], F32, name="ident")
 
         def vec_tile(shape, dtype, name):
@@ -71,6 +74,67 @@ def tile_list_quadrature_motion_readout_kernel(
                 src = w_in[key[0]][a * KP : (a + 1) * KP, b * KP + h * width : b * KP + (h + 1) * width]
                 nc.sync.dma_start(out=r[:], in_=src.rearrange("(p j) r -> p j r", j=PACK))
                 raw[key].append(r)
+
+        def load_group(m, a, g):
+            key = "%s%d%s" % (m, a, "ab"[g])
+            r = ring.tile([P, PACK, PAIR], F32, name="raw" + key, tag="rawg", bufs=RAWG_BUFS, align_bytes=64)
+            src = w_in[m][a * KP : (a + 1) * KP, g * PAIR : (g + 1) * PAIR]
+            nc.sync.dma_start(out=r[:], in_=src.rearrange("(p j) r -> p j r", j=PACK))
+            raw[key] = r
+
+        def cast_group(key, eng):
+            make = sca_tile if eng == "s" else vec_tile
+            grouped[key] = make([P, PACK, P // 2, PACK], BF16, "g" + key)
+            dst = grouped[key][:].rearrange("p t m j -> p m j t")
+            src = raw[key][:].rearrange("p j (m t) -> p m j t", t=PACK)
+            if eng == "v":
+                nc.vector.tensor_copy(out=dst, in_=src)
+            else:
+                nc.scalar.copy(out=dst, in_=src)
+
+        def quant_group(key):
+            c = vec_tile([P, PAIR], U32, "wc" + key)
+            s = keep.tile([P, PAIR], U8, name="ws" + key, align_bytes=64)
+            nc.vector.quantize_mx(out=c[:].bitcast(FP8X4), scales=s[:], in_=grouped[key][:].rearrange("p t m j -> p (t m j)"))
+            codes[key] = c
+            scales[key] = s
+            for v in range(2):
+                codes[(key, v)] = c[:, v * P :]
+                scales[(key, v)] = s[:, v * P :]
+
+        def group_pass(m, g, k, a):
+            key = "%s%d%s" % (m, a, "ab"[g])
+            if a == 0:
+                opened[("g", m, g, k)] = bank([P, 2, PAIR])
+            for jj in range(2):
+                js = slice((2 * k + jj) * P, (2 * k + jj + 1) * P)
+                nc.tensor.matmul_mx(
+                    out=opened[("g", m, g, k)][:, jj, :],
+                    lhsT=v_t[a][:, js].bitcast(FP8X4),
+                    lhsT_scale=vs_t[4 * a : P, js],
+                    rhs=codes[key][:].bitcast(FP8X4),
+                    rhs_scale=scales[key][:],
+                    start=(a == 0 and jj == 0),
+                    stop=(a == 1 and jj == 1),
+                )
+
+        def group_open(m, g, ks=range(4)):
+            for k in ks:
+                group_pass(m, g, k, 0)
+
+        def group_square(m, g, ks=range(4), **bias):
+            for k in ks:
+                if ("g", m, g, k) not in opened:
+                    group_pass(m, g, k, 0)
+                group_pass(m, g, k, 1)
+                if k % 2 == 0:
+                    cols_tiles[("g", m, g, k // 2)] = sca_tile([P, 4, PAIR], F32, "sq%s%d" % (m, g))
+                tile = cols_tiles[("g", m, g, k // 2)]
+                jl = 2 * (k % 2)
+                nc.scalar.activation(out=tile[:, jl : jl + 2, :], in_=opened[("g", m, g, k)][:], func=ACT.Square, **(bias if k == 0 else {}))
+                for jj in range(2):
+                    for v in range(2):
+                        sq[(m, 2 * g + v, 2 * k + jj)] = tile[:, jl + jj, v * P : (v + 1) * P]
 
         def load_tab(a):
             nc.sync.dma_start(out=tab_t[a][:], in_=tab_words[a].rearrange("p t i -> p (t i)").bitcast(I32))
@@ -120,10 +184,14 @@ def tile_list_quadrature_motion_readout_kernel(
 
         opened = {}
 
+        def chunk_of(m, a, u):
+            if u < PACK:
+                return "%s%d%s" % (m, a, "ab"[u // 2]), u % 2
+            return "%s%d1" % (m, a), u - PACK
+
         def rows_pass(acc, m, u, half, a):
-            b, t = divmod(u, PACK)
             cols = slice(half * BANK, (half + 1) * BANK)
-            key = "%s%d%d" % (m, a, b)
+            key, t = chunk_of(m, a, u)
             nc.tensor.matmul_mx(
                 out=acc[:],
                 lhsT=codes[(key, t)][:, :P].bitcast(FP8X4),
@@ -154,9 +222,8 @@ def tile_list_quadrature_motion_readout_kernel(
         cols_tiles = {}
 
         def cols_pass(acc, m, u, count, j, a):
-            b, t = divmod(u, PACK)
             js = slice(j * P, (j + 1) * P)
-            key = "%s%d%d" % (m, a, b)
+            key, t = chunk_of(m, a, u)
             nc.tensor.matmul_mx(
                 out=acc,
                 lhsT=v_t[a][:, js].bitcast(FP8X4),
@@ -257,9 +324,9 @@ def tile_list_quadrature_motion_readout_kernel(
             nc.vector.tensor_copy(out=later[(u, lo)][:], in_=hs[u][:].indirect(pos2_t[:, lo // 16 : hi // 16]))
 
         def pick_first(u, lo=0, hi=NPAIR):
-            b, t = divmod(u, PACK)
+            dst = [diff[0][:, 0, :], diff[0][:, 2, :], spare[:, 0, :], spare[:, 1, :]][u] if u < PACK else diff[1][:, u - PACK, :]
             nc.vector.tensor_tensor(
-                out=diff[b][:, t, lo:hi], in0=hs[u][:].indirect(pos1_t[:, lo // 16 : hi // 16]), in1=later[(u, lo)][:], op=ALU.subtract
+                out=dst[:, lo:hi], in0=hs[u][:].indirect(pos1_t[:, lo // 16 : hi // 16]), in1=later[(u, lo)][:], op=ALU.subtract
             )
 
         zs = {}
@@ -339,12 +406,15 @@ def tile_list_quadrature_motion_readout_kernel(
         load_tab(0)
         load_scales((0, 1))
         nc.sync.dma_start(out=offs_t[:], in_=offs)
-        load_w("e10")
+        load_group("e", 0, 0)
+        load_group("e", 1, 0)
         load_scales((2, 3))
-        load_w("e00")
         load_tab(1)
-        load_w("o00")
-        load_w("o10", 2)
+        load_group("o", 0, 0)
+        load_group("o", 1, 0)
+        for m in "eo":
+            for a in range(2):
+                load_group(m, a, 1)
         nc.sync.dma_start(out=pos2_t[:], in_=pos2)
         nc.sync.dma_start(out=pos1_t[:], in_=pos1)
         for key in ("e01", "e11", "o01", "o11"):
@@ -353,59 +423,66 @@ def tile_list_quadrature_motion_readout_kernel(
 
         gather_tab(0, 0)
         gather_tab(0, 1)
-        cast("e10", "s")
+        cast_group("e0a", "s")
+        cast_group("e1a", "s")
         gather_scales()
-        quant_w("e10")
-        cast("e00", "s")
-        quant_w("e00")
+        quant_group("e0a")
+        quant_group("e1a")
         open_rows("e", 0)
         open_cols("e", 1, 1)
-        open_cols("e", 2, 2)
         gather_tab(1, 0)
         gather_tab(1, 1)
+        cast_group("o0a", "s")
+        cast_group("o1a", "v")
         square_rows("e", 0, (0,), bias=bias0[:])
         square_cols("e", 1, 1, 0, 2)
-        square_cols("e", 2, 2, 0, 2)
         square_rows("e", 0, (1,))
         square_cols("e", 1, 1, 1, 2)
-        cast("o00", "v")
-        square_cols("e", 2, 2, 1, 2)
-        cast("o10", "vv", 0)
-        quant_w("o00", 0, 2)
+        quant_group("o0a")
         open_rows("o", 0)
         open_cols("o", 1, 1)
-        cast("o10", "vv", 1)
-        quant_w("o00", 2, 4)
-        quant_w("o10", 0, 1)
+        quant_group("o1a")
         square_rows("o", 0)
-        quant_w("o10", 1, 2)
         square_cols("o", 1)
-        quant_w("o10", 2, 4)
-        cast_pairs("e01", "v")
+        cast_group("e0b", "v")
+        cast_group("e1b", "v")
+        quant_group("e0b")
+        quant_group("e1b")
         root_rows(0)
-        quant_pairs("e01")
-        square_cols("o", 2, 2)
-        cast_pairs("e11", "v")
         root_cols(1)
+        cast_group("o0b", "v")
+        group_square("e", 1)
+        cast_group("o1b", "v")
+        quant_group("o0b")
+        quant_group("o1b")
+        group_square("o", 1)
+        cast_pairs("e01", "v")
         pick_second(0)
-        quant_pairs("e11")
-        cast_pairs("o01", "v")
+        quant_pairs("e01")
+        root_half(2, 0)
+        root_half(3, 0)
+        root_half(2, 1)
+        root_half(3, 1)
+        cast_pairs("e11", "v")
         pick_first(0)
-        root_cols(2)
-        root_cols(3)
-        quant_pairs("o01")
-        cast_pairs("o11", "v")
-        pick_second(1)
+        quant_pairs("e11")
         square_pair("e", 4)
+        cast_pairs("o01", "v")
+        cast_pairs("o11", "v")
+        quant_pairs("o01")
         quant_pairs("o11")
-        pick_second(2)
-        pick_first(1)
         square_pair("e", 6)
         square_pair("o", 4)
+        pick_second(1)
+        pick_first(1)
+        nc.sync.dma_start(out=diff[0][0:HALF, 1:PACK:2, :], in_=diff[0][HALF:P, 0:PACK:2, :])
+        pick_second(2)
         pick_second(3)
         pick_first(2)
         root_cols(4)
         pick_first(3)
+        nc.sync.dma_start(out=diff[0][HALF:P, 0:PACK:2, :], in_=spare[0:HALF, :, :])
+        nc.sync.dma_start(out=diff[0][HALF:P, 1:PACK:2, :], in_=spare[HALF:P, :, :])
         pick_second(4)
         root_cols(5)
         square_pair("o", 6)
@@ -415,7 +492,7 @@ def tile_list_quadrature_motion_readout_kernel(
         root_cols(6)
         root_cols(7)
         pick_first(5)
-        weave(0, 0, 2 * w, "s")
+        weave(0, 0, 2 * w, "v")
         weave(0, 2 * w, 4 * w, "s")
         pick_second(6, 0, w)
         quant_z(0, 0, 2 * w)

@@ -42,25 +42,25 @@ def tile_list_quadrature_motion_readout_kernel(
         offs_t = keep.tile([P, S // 16], U16, name="offs_t")
         pos1_t = keep.tile([P, NPAIR // 16], U16, name="pos1_t")
         pos2_t = keep.tile([P, NPAIR // 16], U16, name="pos2_t")
-        tab_t = [keep.tile([P, T], I32, name="tab%d" % a, align_bytes=64) for a in range(2)]
-        tabs_t = keep.tile([P, T // 4], I32, name="tabs", align_bytes=64)
-        w2_t = keep.tile([P, 2, 2 * N], U8, name="w2w", align_bytes=64)
-        w2s_t = keep.tile([P, 2, N], U8, name="w2s", align_bytes=64)
-        v_t = [keep.tile([P, S], U32, name="v%d" % a, align_bytes=64) for a in range(2)]
-        vs_t = keep.tile([P, S], U8, name="vs", align_bytes=64)
+        tab_t = [keep.tile([P, T], I32, name="tab%d" % a, align_bytes=256) for a in range(2)]
+        tabs_t = keep.tile([P, T // 4], I32, name="tabs", align_bytes=256)
+        w2_t = keep.tile([P, 2, 2 * N], U8, name="w2w", align_bytes=256)
+        w2s_t = keep.tile([P, 2, N], U8, name="w2s", align_bytes=256)
+        v_t = [keep.tile([P, S], U32, name="v%d" % a, align_bytes=256) for a in range(2)]
+        vs_t = keep.tile([P, S], U8, name="vs", align_bytes=256)
         zero = keep.tile([P, 1], F32, name="zero")
         bias0 = keep.tile([P, 1], F32, name="bias0")
         w_in = {"e": we, "o": wo}
         raw, codes, scales, grouped = {}, {}, {}, {}
-        diff = [keep.tile([P, PACK, NPAIR], F32, name="diff%d" % b, align_bytes=64) for b in range(2)]
-        spare = keep.tile([P, 2, NPAIR], F32, name="spare", align_bytes=64)
+        diff = [keep.tile([P, PACK, NPAIR], F32, name="diff%d" % b, align_bytes=256) for b in range(2)]
+        spare = keep.tile([P, 2, NPAIR], F32, name="spare", align_bytes=256)
         ident = keep.tile([P, P], F32, name="ident")
 
         def vec_tile(shape, dtype, name):
-            return ring.tile(shape, dtype, name=name, tag="vec", bufs=VEC_BUFS, align_bytes=64)
+            return ring.tile(shape, dtype, name=name, tag="vec", bufs=VEC_BUFS, align_bytes=256)
 
         def sca_tile(shape, dtype, name):
-            return ring.tile(shape, dtype, name=name, tag="sca", bufs=SCA_BUFS, align_bytes=64)
+            return ring.tile(shape, dtype, name=name, tag="sca", bufs=SCA_BUFS, align_bytes=256)
 
         def bank(shape):
             return psum.tile(shape, F32, name="acc", tag="acc", bufs=8)
@@ -70,14 +70,14 @@ def tile_list_quadrature_motion_readout_kernel(
             width = KP // parts
             raw[key] = []
             for h in range(parts):
-                r = ring.tile([P, PACK, width], F32, name="raw" + key, tag="raw%d" % parts, bufs=RAW_BUFS if parts == 1 else parts, align_bytes=64)
+                r = ring.tile([P, PACK, width], F32, name="raw" + key, tag="raw%d" % parts, bufs=RAW_BUFS if parts == 1 else parts, align_bytes=256)
                 src = w_in[key[0]][a * KP : (a + 1) * KP, b * KP + h * width : b * KP + (h + 1) * width]
                 nc.sync.dma_start(out=r[:], in_=src.rearrange("(p j) r -> p j r", j=PACK))
                 raw[key].append(r)
 
         def load_group(m, a, g):
             key = "%s%d%s" % (m, a, "ab"[g])
-            r = ring.tile([P, PACK, PAIR], F32, name="raw" + key, tag="rawg", bufs=RAWG_BUFS, align_bytes=64)
+            r = ring.tile([P, PACK, PAIR], F32, name="raw" + key, tag="rawg", bufs=RAWG_BUFS, align_bytes=256)
             src = w_in[m][a * KP : (a + 1) * KP, g * PAIR : (g + 1) * PAIR]
             nc.sync.dma_start(out=r[:], in_=src.rearrange("(p j) r -> p j r", j=PACK))
             raw[key] = r
@@ -94,7 +94,7 @@ def tile_list_quadrature_motion_readout_kernel(
 
         def quant_group(key):
             c = vec_tile([P, PAIR], U32, "wc" + key)
-            s = keep.tile([P, PAIR], U8, name="ws" + key, align_bytes=64)
+            s = keep.tile([P, PAIR], U8, name="ws" + key, align_bytes=256)
             nc.vector.quantize_mx(out=c[:].bitcast(FP8X4), scales=s[:], in_=grouped[key][:].rearrange("p t m j -> p (t m j)"))
             codes[key] = c
             scales[key] = s
@@ -169,7 +169,7 @@ def tile_list_quadrature_motion_readout_kernel(
         def quant_w(key, t0=0, t1=PACK):
             flat = grouped[key][:].rearrange("p t m j -> p (t m j)")
             c = vec_tile([P, (t1 - t0) * P], U32, "wc" + key)
-            s = keep.tile([P, (t1 - t0) * P], U8, name="ws%s%d" % (key, t0), align_bytes=64)
+            s = keep.tile([P, (t1 - t0) * P], U8, name="ws%s%d" % (key, t0), align_bytes=256)
             nc.vector.quantize_mx(out=c[:].bitcast(FP8X4), scales=s[:], in_=flat[:, t0 * KP : t1 * KP])
             for t in range(t0, t1):
                 codes[(key, t)] = c[:, (t - t0) * P :]
@@ -265,8 +265,8 @@ def tile_list_quadrature_motion_readout_kernel(
         def cast_pairs(key, eng="v"):
             make = sca_tile if eng == "s" else vec_tile
             grouped[key] = make([P, 2, P, 2, PACK], BF16, "g" + key)
-            dst = grouped[key][:].rearrange("p u m t j -> p m u j t")
-            src = raw[key][0][:].rearrange("p j (m u t) -> p m u j t", u=2, t=2)
+            dst = grouped[key][:].rearrange("p u m t j -> p m j u t")
+            src = raw[key][0][:].rearrange("p j (m u t) -> p m j u t", u=2, t=2)
             if eng == "v":
                 nc.vector.tensor_copy(out=dst, in_=src)
             else:
@@ -274,7 +274,7 @@ def tile_list_quadrature_motion_readout_kernel(
 
         def quant_pairs(key):
             c = vec_tile([P, KP], U32, "wc" + key)
-            s = keep.tile([P, KP], U8, name="ws" + key, align_bytes=64)
+            s = keep.tile([P, KP], U8, name="ws" + key, align_bytes=256)
             nc.vector.quantize_mx(out=c[:].bitcast(FP8X4), scales=s[:], in_=grouped[key][:].rearrange("p u m t j -> p (u m t j)"))
             for t in (0, 2):
                 codes[(key, t)] = c[:, t * P :]
@@ -348,7 +348,7 @@ def tile_list_quadrature_motion_readout_kernel(
 
         def quant_z(b, lo, hi):
             c = vec_tile([P, hi - lo], U32, "zc%d" % b)
-            s = keep.tile([P, hi - lo], U8, name="zs%d_%d" % (b, lo), align_bytes=64)
+            s = keep.tile([P, hi - lo], U8, name="zs%d_%d" % (b, lo), align_bytes=256)
             nc.vector.quantize_mx(out=c[:].bitcast(FP8X4), scales=s[:], in_=zs[(b, lo)][:])
             for c0 in range(lo, hi, P):
                 z_codes[(b, c0)] = c[:, c0 - lo : c0 - lo + P]

from contextlib import ExitStack

import concourse.mybir as mybir
from concourse.masks import make_identity

K, T, S, NPAIR, H, N = 1024, 4096, 1024, 512, 1024, 512
FLOPS = 2 * 2 * K * H * S + 2 * H * N * NPAIR

F32 = mybir.dt.float32
BF16 = mybir.dt.bfloat16
I32 = mybir.dt.int32
U32 = mybir.dt.uint32
U16 = mybir.dt.uint16
U8 = mybir.dt.uint8
FP8X4 = mybir.dt.float8_e4m3fn_x4
FP4X4 = mybir.dt.float4_e2m1fn_x4
ACT = mybir.ActivationFunctionType
ALU = mybir.AluOpType

P = 128
PACK = 4
KP = P * PACK
BANK = 512
RAW_BUFS = 3
RAWG_BUFS = 5
VEC_BUFS = 15
SCA_BUFS = 12
PIECES = 4
PAIR = 2 * P
HALF = P // 2


def tile_list_quadrature_motion_readout_kernel(
    tc, tab_words, tab_scales, offs, we, wo, pos1, pos2, w2_words, w2_scales, out
):
    nc = tc.nc
    with ExitStack() as ctx:
        keep = ctx.enter_context(tc.tile_pool(name="keep", bufs=1))
        ring = ctx.enter_context(tc.tile_pool(name="ring", bufs=2))
        psum = ctx.enter_context(tc.psum_pool(name="psum", bufs=8))

        offs_t = keep.tile([P, S // 16], U16, name="offs_t")
        pos1_t = keep.tile([P, NPAIR // 16], U16, name="pos1_t")
        pos2_t = keep.tile([P, NPAIR // 16], U16, name="pos2_t")
        tab_t = [keep.tile([P, T], I32, name="tab%d" % a, align_bytes=256) for a in range(2)]
        tabs_t = keep.tile([P, T // 4], I32, name="tabs", align_bytes=256)
        w2_t = keep.tile([P, 2, 2 * N], U8, name="w2w", align_bytes=256)
        w2s_t = keep.tile([P, 2, N], U8, name="w2s", align_bytes=256)
        v_t = [keep.tile([P, S], U32, name="v%d" % a, align_bytes=256) for a in range(2)]
        vs_t = keep.tile([P, S], U8, name="vs", align_bytes=256)
        zero = keep.tile([P, 1], F32, name="zero")
        bias0 = keep.tile([P, 1], F32, name="bias0")
        w_in = {"e": we, "o": wo}
        raw, codes, scales, grouped = {}, {}, {}, {}
        diff = [keep.tile([P, PACK, NPAIR], F32, name="diff%d" % b, align_bytes=256) for b in range(2)]
        spare = keep.tile([P, 2, NPAIR], F32, name="spare", align_bytes=256)
        ident = keep.tile([P, P], F32, name="ident")

        def vec_tile(shape, dtype, name):
            return ring.tile(shape, dtype, name=name, tag="vec", bufs=VEC_BUFS, align_bytes=256)

        def sca_tile(shape, dtype, name):
            return ring.tile(shape, dtype, name=name, tag="sca", bufs=SCA_BUFS, align_bytes=256)

        def bank(shape):
            return psum.tile(shape, F32, name="acc", tag="acc", bufs=8)

        def load_w(key, parts=1):
            a, b = int(key[1]), int(key[2])
            width = KP // parts
            raw[key] = []
            for h in range(parts):
                r = ring.tile([P, PACK, width], F32, name="raw" + key, tag="raw%d" % parts, bufs=RAW_BUFS if parts == 1 else parts, align_bytes=256)
                src = w_in[key[0]][a * KP : (a + 1) * KP, b * KP + h * width : b * KP + (h + 1) * width]
                nc.sync.dma_start(out=r[:], in_=src.rearrange("(p j) r -> p j r", j=PACK))
                raw[key].append(r)

        def load_group(m, a, g):
            key = "%s%d%s" % (m, a, "ab"[g])
            r = ring.tile([P, PACK, PAIR], F32, name="raw" + key, tag="rawg", bufs=RAWG_BUFS, align_bytes=256)
            src = w_in[m][a * KP : (a + 1) * KP, g * PAIR : (g + 1) * PAIR]
            nc.sync.dma_start(out=r[:], in_=src.rearrange("(p j) r -> p j r", j=PACK))
            raw[key] = r

        def cast_group(key, eng):
            make = sca_tile if eng == "s" else vec_tile
            grouped[key] = make([P, PACK, P // 2, PACK], BF16, "g" + key)
            dst = grouped[key][:].rearrange("p t m j -> p m j t")
            src = raw[key][:].rearrange("p j (m t) -> p m j t", t=PACK)
            if eng == "v":
                nc.vector.tensor_copy(out=dst, in_=src)
            else:
                nc.scalar.copy(out=dst, in_=src)

        def quant_group(key):
            c = vec_tile([P, PAIR], U32, "wc" + key)
            s = keep.tile([P, PAIR], U8, name="ws" + key, align_bytes=256)
            nc.vector.quantize_mx(out=c[:].bitcast(FP8X4), scales=s[:], in_=grouped[key][:].rearrange("p t m j -> p (t m j)"))
            codes[key] = c
            scales[key] = s
            for v in range(2):
                codes[(key, v)] = c[:, v * P :]
                scales[(key, v)] = s[:, v * P :]

        def group_pass(m, g, k, a):
            key = "%s%d%s" % (m, a, "ab"[g])
            if a == 0:
                opened[("g", m, g, k)] = bank([P, 2, PAIR])
            for jj in range(2):
                js = slice((2 * k + jj) * P, (2 * k + jj + 1) * P)
                nc.tensor.matmul_mx(
                    out=opened[("g", m, g, k)][:, jj, :],
                    lhsT=v_t[a][:, js].bitcast(FP8X4),
                    lhsT_scale=vs_t[4 * a : P, js],
                    rhs=codes[key][:].bitcast(FP8X4),
                    rhs_scale=scales[key][:],
                    start=(a == 0 and jj == 0),
                    stop=(a == 1 and jj == 1),
                )

        def group_open(m, g, ks=range(4)):
            for k in ks:
                group_pass(m, g, k, 0)

        def group_square(m, g, ks=range(4), **bias):
            for k in ks:
                if ("g", m, g, k) not in opened:
                    group_pass(m, g, k, 0)
                group_pass(m, g, k, 1)
                if k % 2 == 0:
                    cols_tiles[("g", m, g, k // 2)] = sca_tile([P, 4, PAIR], F32, "sq%s%d" % (m, g))
                tile = cols_tiles[("g", m, g, k // 2)]
                jl = 2 * (k % 2)
                nc.scalar.activation(out=tile[:, jl : jl + 2, :], in_=opened[("g", m, g, k)][:], func=ACT.Square, **(bias if k == 0 else {}))
                for jj in range(2):
                    for v in range(2):
                        sq[(m, 2 * g + v, 2 * k + jj)] = tile[:, jl + jj, v * P : (v + 1) * P]

        def load_tab(a):
            nc.sync.dma_start(out=tab_t[a][:], in_=tab_words[a].rearrange("p t i -> p (t i)").bitcast(I32))

        def load_scales(rows):
            for r in rows:
                for a in range(2):
                    nc.sync.dma_start(out=tabs_t[4 * a + r : P : 32, :], in_=tab_scales[a, r:16:4, :].bitcast(I32))

        def cast(key, engines, only=None):
            make = sca_tile if engines[0] == "s" else vec_tile
            if key not in grouped:
                grouped[key] = make([P, PACK, P, PACK], BF16, "g" + key)
            g = grouped[key]
            rows = P // len(engines)
            per_load = P // len(raw[key])
            for h, eng in enumerate(engines):
                if only is not None and h != only:
                    continue
                m0 = h * rows
                r = raw[key][m0 // per_load]
                c0 = (m0 % per_load) * PACK
                dst = g[:, :, m0 : m0 + rows, :].rearrange("p t m j -> p m j t")
                src = r[:, :, c0 : c0 + rows * PACK].rearrange("p j (m t) -> p m j t", t=PACK)
                if eng == "v":
                    nc.vector.tensor_copy(out=dst, in_=src)
                elif eng == "s":
                    nc.scalar.copy(out=dst, in_=src)
                else:
                    nc.gpsimd.tensor_scalar(out=dst, in0=src, scalar1=1.0, scalar2=0.0, op0=ALU.mult, op1=ALU.add)

        def quant_w(key, t0=0, t1=PACK):
            flat = grouped[key][:].rearrange("p t m j -> p (t m j)")
            c = vec_tile([P, (t1 - t0) * P], U32, "wc" + key)
            s = keep.tile([P, (t1 - t0) * P], U8, name="ws%s%d" % (key, t0), align_bytes=256)
            nc.vector.quantize_mx(out=c[:].bitcast(FP8X4), scales=s[:], in_=flat[:, t0 * KP : t1 * KP])
            for t in range(t0, t1):
                codes[(key, t)] = c[:, (t - t0) * P :]
                scales[(key, t)] = s[:, (t - t0) * P :]

        def gather_tab(a, half):
            cols = slice(half * BANK, (half + 1) * BANK)
            lst = offs_t[:, half * BANK // 16 : (half + 1) * BANK // 16]
            nc.vector.tensor_copy(out=v_t[a][:, cols], in_=tab_t[a][:].bitcast(U32).indirect(lst))

        sq, hs = {}, {}

        opened = {}

        def chunk_of(m, a, u):
            if u < PACK:
                return "%s%d%s" % (m, a, "ab"[u // 2]), u % 2
            return "%s%d1" % (m, a), u - PACK

        def rows_pass(acc, m, u, half, a):
            cols = slice(half * BANK, (half + 1) * BANK)
            key, t = chunk_of(m, a, u)
            nc.tensor.matmul_mx(
                out=acc[:],
                lhsT=codes[(key, t)][:, :P].bitcast(FP8X4),
                lhsT_scale=scales[(key, t)][:, :P],
                rhs=v_t[a][:, cols].bitcast(FP8X4),
                rhs_scale=vs_t[4 * a : P, cols],
                start=(a == 0),
                stop=(a == 1),
            )

        def open_rows(m, u):
            for half in range(2):
                opened[(m, u, half)] = bank([P, BANK])
                rows_pass(opened[(m, u, half)], m, u, half, 0)

        def square_rows(m, u, halves=(0, 1), **bias):
            if 0 in halves:
                sq[(m, u)] = sca_tile([P, S], F32, "sq%s%d" % (m, u))
            for half in halves:
                if (m, u, half) in opened:
                    acc = opened[(m, u, half)]
                else:
                    acc = bank([P, BANK])
                    rows_pass(acc, m, u, half, 0)
                rows_pass(acc, m, u, half, 1)
                nc.scalar.activation(out=sq[(m, u)][:, half * BANK : (half + 1) * BANK], in_=acc[:], func=ACT.Square, **bias)

        cols_tiles = {}

        def cols_pass(acc, m, u, count, j, a):
            js = slice(j * P, (j + 1) * P)
            key, t = chunk_of(m, a, u)
            nc.tensor.matmul_mx(
                out=acc,
                lhsT=v_t[a][:, js].bitcast(FP8X4),
                lhsT_scale=vs_t[4 * a : P, js],
                rhs=codes[(key, t)][:, : count * P].bitcast(FP8X4),
                rhs_scale=scales[(key, t)][:, : count * P],
                start=(a == 0),
                stop=(a == 1),
            )

        def cols_square(acc, m, u, count, j0, **bias):
            per = PACK // count
            c, jl = divmod(j0, 2 * per)
            if jl == 0:
                cols_tiles[(m, u, c)] = sca_tile([P, 2 * per, count * P], F32, "sq%s%d" % (m, u))
            tile = cols_tiles[(m, u, c)]
            nc.scalar.activation(out=tile[:, jl : jl + per, :], in_=acc[:], func=ACT.Square, **bias)
            for d in range(count):
                for jj in range(per):
                    sq[(m, u + d, j0 + jj)] = tile[:, jl + jj, d * P : (d + 1) * P]

        def open_cols(m, u, count):
            per = PACK // count
            for j0 in range(0, S // P, per):
                opened[(m, u, j0)] = bank([P, per, count * P])
                cols_pass(opened[(m, u, j0)][:, 0, :], m, u, count, j0, 0)

        def square_cols(m, u, count=1, part=0, parts=1, **bias):
            per = PACK // count
            span = S // P // parts
            for j0 in range(part * span, (part + 1) * span, per):
                ahead = (m, u, j0) in opened
                acc = opened[(m, u, j0)] if ahead else bank([P, per, count * P])
                for jj in range(per):
                    for a in range(1 if ahead and jj == 0 else 0, 2):
                        cols_pass(acc[:, jj, :], m, u, count, j0 + jj, a)
                cols_square(acc, m, u, count, j0, **bias)

        def cast_pairs(key, eng="v"):
            make = sca_tile if eng == "s" else vec_tile
            grouped[key] = make([P, 2, P, 2, PACK], BF16, "g" + key)
            dst = grouped[key][:].rearrange("p u m t j -> p m j u t")
            src = raw[key][0][:].rearrange("p j (m u t) -> p m j u t", u=2, t=2)
            if eng == "v":
                nc.vector.tensor_copy(out=dst, in_=src)
            else:
                nc.scalar.copy(out=dst, in_=src)

        def quant_pairs(key):
            c = vec_tile([P, KP], U32, "wc" + key)
            s = keep.tile([P, KP], U8, name="ws" + key, align_bytes=256)
            nc.vector.quantize_mx(out=c[:].bitcast(FP8X4), scales=s[:], in_=grouped[key][:].rearrange("p u m t j -> p (u m t j)"))
            for t in (0, 2):
                codes[(key, t)] = c[:, t * P :]
                scales[(key, t)] = s[:, t * P :]

        def square_pair(m, u):
            for half in range(2):
                tile = sca_tile([P, 4, 2, P], F32, "sq%s%d" % (m, u))
                for jl in (0, 2):
                    acc = bank([P, 2, PAIR])
                    for jj in range(2):
                        for a in range(2):
                            cols_pass(acc[:, jj, :], m, u, 2, 4 * half + jl + jj, a)
                    nc.scalar.activation(out=tile[:, jl : jl + 2, :, :], in_=acc[:].rearrange("p j (m t) -> p j t m", t=2), func=ACT.Square)
                for jl in range(4):
                    for t in range(2):
                        sq[(m, u + t, 4 * half + jl)] = tile[:, jl, t, :]

        def root_half(u, half):
            if half == 0:
                hs[u] = sca_tile([P, S], F32, "h%d" % u)
            acc = bank([P, BANK])
            for j0 in range(0, BANK, P):
                jt = (half * BANK + j0) // P
                nc.tensor.matmul(acc[:, j0 : j0 + P], sq[("e", u, jt)], ident[:], start=True, stop=False, is_transpose=True)
                nc.tensor.matmul(acc[:, j0 : j0 + P], sq[("o", u, jt)], ident[:], start=False, stop=True, is_transpose=True)
            nc.scalar.activation(out=hs[u][:, half * BANK : (half + 1) * BANK], in_=acc[:], func=ACT.Sqrt)

        def root_cols(u):
            root_half(u, 0)
            root_half(u, 1)

        def root_rows(u, parts=2, eng="v"):
            ss = vec_tile([P, S], F32, "ss%d" % u)
            hs[u] = sca_tile([P, S], F32, "h%d" % u)
            w = S // parts
            for c in range(parts):
                cols = slice(c * w, (c + 1) * w)
                adder = nc.vector if eng == "v" else nc.gpsimd
                adder.tensor_tensor(out=ss[:, cols], in0=sq[("e", u)][:, cols], in1=sq[("o", u)][:, cols], op=ALU.add)
                nc.scalar.activation(out=hs[u][:, cols], in_=ss[:, cols], func=ACT.Sqrt)

        later = {}

        def pick_second(u, lo=0, hi=NPAIR):
            later[(u, lo)] = vec_tile([P, hi - lo], F32, "hb%d" % u)
            nc.vector.tensor_copy(out=later[(u, lo)][:], in_=hs[u][:].indirect(pos2_t[:, lo // 16 : hi // 16]))

        def pick_first(u, lo=0, hi=NPAIR):
            dst = [diff[0][:, 0, :], diff[0][:, 2, :], spare[:, 0, :], spare[:, 1, :]][u] if u < PACK else diff[1][:, u - PACK, :]
            nc.vector.tensor_tensor(
                out=dst[:, lo:hi], in0=hs[u][:].indirect(pos1_t[:, lo // 16 : hi // 16]), in1=later[(u, lo)][:], op=ALU.subtract
            )

        zs = {}

        def weave(b, lo, hi, eng):
            make = sca_tile if eng == "s" else vec_tile
            z = make([P, (hi - lo) * PACK], BF16, "z%d" % b)
            zs[(b, lo)] = z
            dst = z[:].rearrange("p (c i t) -> p c t i", i=4, t=PACK)
            src = diff[b][:, :, lo:hi].rearrange("p t (c i) -> p c t i", i=4)
            if eng == "s":
                nc.scalar.copy(out=dst, in_=src)
            elif eng == "v":
                nc.vector.tensor_copy(out=dst, in_=src)
            else:
                nc.gpsimd.tensor_scalar(out=dst, in0=src, scalar1=1.0, scalar2=0.0, op0=ALU.mult, op1=ALU.add)

        z_codes, z_scales = {}, {}

        def quant_z(b, lo, hi):
            c = vec_tile([P, hi - lo], U32, "zc%d" % b)
            s = keep.tile([P, hi - lo], U8, name="zs%d_%d" % (b, lo), align_bytes=256)
            nc.vector.quantize_mx(out=c[:].bitcast(FP8X4), scales=s[:], in_=zs[(b, lo)][:])
            for c0 in range(lo, hi, P):
                z_codes[(b, c0)] = c[:, c0 - lo : c0 - lo + P]
                z_scales[(b, c0)] = s[:, c0 - lo : c0 - lo + P]

        out_v = out.rearrange("(g p) i -> p g i", p=P)

        def w2_pass(acc, g, a, c0):
            nc.tensor.matmul_mx(
                out=acc,
                lhsT=w2_t[:, a, 2 * g * P : 2 * (g + 1) * P].bitcast(FP4X4),
                lhsT_scale=w2s_t[:, a, g * P : (g + 1) * P],
                rhs=z_codes[(a, c0)].bitcast(FP8X4),
                rhs_scale=z_scales[(a, c0)],
                start=(a == 0),
                stop=(a == 1),
            )

        def readout(lo):
            res = sca_tile([P, N // P, P], F32, "res")
            acc = bank([P, N // P, P])
            for g in range(N // P):
                for a in range(2):
                    w2_pass(acc[:, g, :], g, a, lo)
            nc.scalar.copy(out=res[:], in_=acc[:])
            nc.sync.dma_start(out=out_v[:, :, lo : lo + P], in_=res[:])

        def readout_last(lo, accs):
            res = sca_tile([P, N // P, P], F32, "res")
            for g in range(N // P):
                w2_pass(accs[g][:], g, 1, lo)
                if g % 2 == 0:
                    nc.scalar.copy(out=res[:, g, :], in_=accs[g][:])
                else:
                    nc.vector.tensor_copy(out=res[:, g, :], in_=accs[g][:])
                    nc.sync.dma_start(out=out_v[:, g - 1 : g + 1, lo : lo + P], in_=res[:, g - 1 : g + 1, :])

        def load_w2():
            nc.sync.dma_start(out=w2_t[:].bitcast(I32), in_=w2_words.rearrange("a p c -> p a c").bitcast(I32))
            for q in range(4):
                nc.sync.dma_start(
                    out=w2s_t[32 * q : 32 * q + 4, :, :].bitcast(I32),
                    in_=w2_scales[:, 4 * q : 4 * q + 4, :].rearrange("a r n -> r a n").bitcast(I32),
                )

        def gather_scales():
            nc.vector.tensor_copy(out=vs_t[:], in_=tabs_t[:].bitcast(U8).indirect(offs_t[:]))

        make_identity(nc, ident[:])
        nc.vector.memset(tabs_t[:], 0)
        nc.vector.memset(zero[:], 0.0)
        nc.vector.memset(w2s_t[:].rearrange("p a n -> p (a n)").bitcast(I32), 0)
        nc.scalar.activation(out=bias0[:], in_=zero[:], func=ACT.Sqrt)

        load_tab(0)
        load_scales((0, 1))
        nc.sync.dma_start(out=offs_t[:], in_=offs)
        load_group("e", 0, 0)
        load_group("e", 1, 0)
        load_scales((2, 3))
        load_tab(1)
        load_group("o", 0, 0)
        load_group("o", 1, 0)
        for m in "eo":
            for a in range(2):
                load_group(m, a, 1)
        nc.sync.dma_start(out=pos2_t[:], in_=pos2)
        nc.sync.dma_start(out=pos1_t[:], in_=pos1)
        for key in ("e01", "e11", "o01", "o11"):
            load_w(key)
        load_w2()

        gather_tab(0, 0)
        gather_tab(0, 1)
        cast_group("e0a", "s")
        cast_group("e1a", "s")
        gather_scales()
        quant_group("e0a")
        quant_group("e1a")
        open_rows("e", 0)
        open_cols("e", 1, 1)
        gather_tab(1, 0)
        gather_tab(1, 1)
        cast_group("o0a", "s")
        cast_group("o1a", "v")
        square_rows("e", 0, (0,), bias=bias0[:])
        square_cols("e", 1, 1, 0, 2)
        square_rows("e", 0, (1,))
        square_cols("e", 1, 1, 1, 2)
        quant_group("o0a")
        open_rows("o", 0)
        open_cols("o", 1, 1)
        quant_group("o1a")
        square_rows("o", 0)
        square_cols("o", 1)
        cast_group("e0b", "v")
        cast_group("e1b", "v")
        quant_group("e0b")
        quant_group("e1b")
        root_rows(0)
        root_cols(1)
        cast_group("o0b", "v")
        group_square("e", 1)
        cast_group("o1b", "v")
        quant_group("o0b")
        quant_group("o1b")
        group_square("o", 1)
        cast_pairs("e01", "v")
        pick_second(0)
        quant_pairs("e01")
        root_half(2, 0)
        root_half(3, 0)
        root_half(2, 1)
        root_half(3, 1)
        cast_pairs("e11", "v")
        pick_first(0)
        quant_pairs("e11")
        square_pair("e", 4)
        cast_pairs("o01", "v")
        cast_pairs("o11", "v")
        quant_pairs("o01")
        quant_pairs("o11")
        square_pair("e", 6)
        square_pair("o", 4)
        pick_second(1)
        pick_first(1)
        nc.sync.dma_start(out=diff[0][0:HALF, 1:PACK:2, :], in_=diff[0][HALF:P, 0:PACK:2, :])
        pick_second(2)
        pick_second(3)
        pick_first(2)
        root_cols(4)
        pick_first(3)
        nc.sync.dma_start(out=diff[0][HALF:P, 0:PACK:2, :], in_=spare[0:HALF, :, :])
        nc.sync.dma_start(out=diff[0][HALF:P, 1:PACK:2, :], in_=spare[HALF:P, :, :])
        pick_second(4)
        root_cols(5)
        square_pair("o", 6)
        w = NPAIR // PIECES
        pick_second(5)
        pick_first(4)
        root_cols(6)
        root_cols(7)
        pick_first(5)
        weave(0, 0, 2 * w, "v")
        weave(0, 2 * w, 4 * w, "s")
        pick_second(6, 0, w)
        quant_z(0, 0, 2 * w)
        for c in range(PIECES):
            lo, hi = c * w, (c + 1) * w
            pick_second(7, lo, hi)
            pick_first(6, lo, hi)
            if c + 1 < PIECES:
                pick_second(6, hi, hi + w)
            pick_first(7, lo, hi)
            if c == 1:
                quant_z(0, 2 * w, 4 * w)
                accs = [bank([P, P]) for g in range(N // P)]
                for g in range(N // P):
                    w2_pass(accs[g][:], g, 0, NPAIR - P)
            if c + 1 < PIECES:
                weave(1, lo, hi, "s")
            if c > 0:
                quant_z(1, lo - w, lo)
            if c > 1:
                readout(lo - 2 * w)
        weave(1, NPAIR - w, NPAIR, "v")
        readout(NPAIR - 2 * w)
        quant_z(1, NPAIR - w, NPAIR)
        readout_last(NPAIR - w, accs)
